import numpy as np
import ml_dtypes


def mxq(x, axis, fmt="e4m3"):
    dtype, down = {"e4m3": (ml_dtypes.float8_e4m3fn, 7), "e5m2": (ml_dtypes.float8_e5m2, 14)}[fmt]
    v = np.moveaxis(np.asarray(x, np.float32).astype(ml_dtypes.bfloat16).astype(np.float64), axis, -1)
    blocks = v.reshape(v.shape[:-1] + (-1, 32))
    amax = np.abs(blocks).max(-1, keepdims=True)
    byte = np.maximum(np.where(amax > 0, np.frexp(amax)[1] - 1 + 127, 0) - down, 1)
    scale = np.exp2(byte - 127.0)
    codes = (blocks / scale).astype(np.float32).astype(dtype).astype(np.float64)
    return np.moveaxis((codes * scale).reshape(v.shape), -1, axis)


WIDE = False


def mx_kscale(k):
    if not WIDE:
        return np.ones(k)
    levels = np.array([10, -10, 5, -5, 0])
    if k % 512:
        return np.exp2(np.random.permutation(np.resize(levels, k // 32))).repeat(32)
    a = np.empty((k // 512, 16))
    for p in range(k // 512):
        a[p, :8] = np.random.permutation(np.resize(levels, 8))
        for g in range(8):
            far = levels[np.abs(levels - a[p, g]) >= 10]
            a[p, g + 8] = far[np.random.randint(len(far))]
    return np.exp2(a.ravel()).repeat(32)


def f64(x):
    return np.asarray(x).astype(np.float64)


def striped(idx):
    return np.tile(idx.reshape(-1, 16).T, (8, 1)).astype(np.uint16)


def unstriped(offs):
    return offs[:16].T.reshape(-1).astype(np.int64)


E2M1 = np.array([0.0, 0.5, 1.0, 1.5, 2.0, 3.0, 4.0, 6.0, -0.0, -0.5, -1.0, -1.5, -2.0, -3.0, -4.0, -6.0])


def pack_weight(w, fmt):
    k, n = w.shape
    w = f64(np.asarray(w, np.float32).astype(ml_dtypes.bfloat16)).reshape(k // 32, 32, n)
    amax = np.abs(w).max(1)
    if fmt == "e4m3":
        byte = np.frexp(amax)[1] - 1 + 127 - 7
    else:
        mant, ex = np.frexp(amax / 6.0)
        byte = np.where(mant > 0.5, ex, ex - 1) + 127
    byte = np.clip(np.where(amax > 0, byte, 1), 1, 254)
    scaled = (w * np.exp2(127.0 - byte)[:, None, :]).reshape(k, n).astype(np.float32)
    by_word = np.ascontiguousarray(scaled.reshape(k // 512, 128, 4, n).transpose(0, 1, 3, 2))
    if fmt == "e4m3":
        words = by_word.astype(ml_dtypes.float8_e4m3fn).view(np.uint8)
    else:
        c = by_word.astype(ml_dtypes.float4_e2m1fn).view(np.uint8) & 0xF
        words = (c[..., 0::2] | (c[..., 1::2] << 4)).reshape(k // 512, 128, 2 * n)
    return np.ascontiguousarray(words), np.ascontiguousarray(byte.astype(np.uint8).reshape(k // 512, 16, n))


def unpack_weight(words, scales, fmt):
    g, _, n = scales.shape
    words = np.ascontiguousarray(words).reshape(g, 128, n, -1)
    if fmt == "e4m3":
        vals = words.view(ml_dtypes.float8_e4m3fn).astype(np.float64)
    else:
        nib = np.empty((g, 128, n, 4), np.uint8)
        nib[..., 0::2] = words & 0xF
        nib[..., 1::2] = words >> 4
        vals = E2M1[nib]
    vals = vals * np.repeat(np.exp2(scales.astype(np.float64) - 127.0), 8, axis=1)[..., None]
    return vals.transpose(0, 1, 3, 2).reshape(g * 512, n)


def relu(v):
    return np.maximum(v, 0.0)


K, T, E, C, H, N = 512, 512, 8, 128, 512, 256


def by_expert(wq, xq):
    return np.concatenate([wq[e].T @ xq[:, e * C:(e + 1) * C] for e in range(E)], axis=1)


def setup_inputs():
    n = np.random.standard_normal
    s = mx_kscale(K)
    u = mx_kscale(H)
    first = np.random.permutation(np.repeat(np.arange(E), T // E))
    second = (first + 1 + np.random.permutation(np.repeat(np.arange(E - 1), -(-T // (E - 1)))[:T])) % E
    while np.bincount(second, minlength=E).max() != T // E:
        load = np.bincount(second, minlength=E); hi, lo = int(load.argmax()), int(load.argmin())
        t = np.flatnonzero((second == hi) & (first != lo))[0]; second[t] = lo
    slot_token = np.empty(E * C, np.int64); pos = np.empty((2, T), np.int64); fill = np.zeros(E, np.int64)
    place = np.stack([np.random.permutation(C) for _ in range(E)])
    for r, deal in enumerate((first, second)):
        for t in np.random.permutation(T):
            e = deal[t]; j = e * C + place[e, fill[e]]; fill[e] += 1; slot_token[j] = t; pos[r, t] = j
    g = np.random.uniform(0.2, 0.8, T)
    x = pack_weight(n((K, T)) * s[:, None], "e4m3")
    w = pack_weight(n((K, N)) / np.sqrt(K) / s[:, None], "e4m3")
    wa = [pack_weight(m, "e2m1") for m in n((E, K, H)) / np.sqrt(K) / s[None, :, None] * u]
    wb = [pack_weight(m, "e2m1") for m in n((E, H, N)) / np.sqrt(H) / u[None, :, None]]
    return {
        "x_words": x[0],
        "x_scales": x[1],
        "w_words": w[0],
        "w_scales": w[1],
        "wa_words": np.stack([m[0] for m in wa]),
        "wa_scales": np.stack([m[1] for m in wa]),
        "wb_words": np.stack([m[0] for m in wb]),
        "wb_scales": np.stack([m[1] for m in wb]),
        "gate": np.stack([np.tile(g, (128, 1)), np.tile(1.0 - g, (128, 1))]).astype(np.float32),
        "offs": striped(slot_token),
        "pos1": striped(pos[0]),
        "pos2": striped(pos[1]),
    }


def reference(x_words, x_scales, w_words, w_scales, wa_words, wa_scales, wb_words, wb_scales, gate, offs, pos1, pos2):
    w = unpack_weight(w_words, w_scales, "e4m3")
    wa = np.stack([unpack_weight(wa_words[e], wa_scales[e], "e2m1") for e in range(E)])
    wb = np.stack([unpack_weight(wb_words[e], wb_scales[e], "e2m1") for e in range(E)])
    idx = unstriped(offs)
    x = unpack_weight(x_words, x_scales, "e4m3")
    base = w.T @ x
    h = relu(by_expert(wa, x[:, idx]))
    y = by_expert(wb, mxq(h, 0, "e4m3"))
    c = sum(f64(gate[r, :1]) * y[:, unstriped(p)] for r, p in enumerate((pos1, pos2)))
    return base + c

@@ -1,0 +1,215 @@
+from contextlib import ExitStack
+
+import concourse.mybir as mybir
+from concourse.masks import make_identity
+
+K, T, E, C, H, N = 512, 512, 8, 128, 512, 256
+S = E * C
+FLOPS = 2 * K * N * T + 2 * K * H * S + 2 * H * N * S
+
+F32 = mybir.dt.float32
+BF16 = mybir.dt.bfloat16
+I32 = mybir.dt.int32
+U32 = mybir.dt.uint32
+U16 = mybir.dt.uint16
+U8 = mybir.dt.uint8
+FP8X4 = mybir.dt.float8_e4m3fn_x4
+FP4X4 = mybir.dt.float4_e2m1fn_x4
+MULT = mybir.AluOpType.mult
+ADD = mybir.AluOpType.add
+RELU = mybir.ActivationFunctionType.Relu
+
+P = 128
+PER_COL = 16
+
+
+def load_scale_rows(nc, plane, rows):
+    for q in range(4):
+        nc.sync.dma_start(
+            out=plane[32 * q : 32 * q + 4, :, :].bitcast(I32),
+            in_=rows[:, 4 * q : 4 * q + 4, :].rearrange("g r c -> r g c").bitcast(I32),
+        )
+
+
+def tile_moe_adp_relu_kernel(
+    tc, x_words, x_scales, w_words, w_scales, wa_words, wa_scales, wb_words, wb_scales, gate, offs, pos1, pos2, out
+):
+    nc = tc.nc
+    with ExitStack() as ctx:
+        keep = ctx.enter_context(tc.tile_pool(name="keep", bufs=1))
+        hpool = ctx.enter_context(tc.psum_pool(name="hpool", bufs=2))
+        tpool = ctx.enter_context(tc.psum_pool(name="tpool", bufs=2))
+        ypool = ctx.enter_context(tc.psum_pool(name="ypool", bufs=1))
+
+        offs_t = keep.tile([P, S // PER_COL], U16, name="offs_t")
+        pos1_t = keep.tile([P, T // PER_COL], U16, name="pos1_t")
+        pos2_t = keep.tile([P, T // PER_COL], U16, name="pos2_t")
+        xw = keep.tile([P, T], U32, name="xw", align_bytes=64)
+        xs = keep.tile([P, 1, T], U8, name="xs", align_bytes=64)
+        ww = keep.tile([P, N], U32, name="ww", align_bytes=64)
+        ws = keep.tile([P, 1, N], U8, name="ws", align_bytes=64)
+        was = keep.tile([P, E, H], U8, name="was", align_bytes=64)
+        wbs = keep.tile([P, E, N], U8, name="wbs", align_bytes=64)
+        wbw = keep.tile([P, E, 2 * N], U8, name="wbw", align_bytes=64)
+        gate_t = keep.tile([P, 2, T], F32, name="gate_t")
+        ident = keep.tile([P, P], F32, name="ident")
+        wa_cuts = [(0, 2), (2, 4), (4, 8)]
+        waw_t = [keep.tile([P, b - a, 2 * H], U8, name="waw%d" % a, align_bytes=64) for a, b in wa_cuts]
+        waw = {}
+        for (a, b), tl in zip(wa_cuts, waw_t):
+            for e in range(a, b):
+                waw[e] = tl[:, e - a, :]
+
+        def load_wa(i, eng):
+            a, b = wa_cuts[i]
+            eng.dma_start(out=waw_t[i][:].bitcast(I32), in_=wa_words[a:b, 0].rearrange("e p c -> p e c").bitcast(I32))
+
+        for plane in (xs, was, wbs, ws):
+            nc.vector.memset(plane[:].bitcast(I32), 0)
+
+        nc.sync.dma_start(offs_t[:], offs)
+        nc.scalar.dma_start(out=xw[:].bitcast(I32), in_=x_words[0].rearrange("p t d -> p (t d)").bitcast(I32))
+        load_scale_rows(nc, xs, x_scales)
+        load_wa(0, nc.scalar)
+        load_scale_rows(nc, was, wa_scales[:, 0])
+        load_wa(1, nc.sync)
+        load_wa(2, nc.sync)
+        nc.sync.dma_start(out=wbw[:].bitcast(I32), in_=wb_words[:, 0].rearrange("e p c -> p e c").bitcast(I32))
+        load_scale_rows(nc, wbs, wb_scales[:, 0])
+        nc.sync.dma_start(out=ww[:].bitcast(I32), in_=w_words[0].rearrange("p n d -> p (n d)").bitcast(I32))
+        load_scale_rows(nc, ws, w_scales)
+        nc.sync.dma_start(out=gate_t[:], in_=gate.rearrange("r p t -> p r t"))
+        nc.sync.dma_start(pos1_t[:], pos1)
+        nc.sync.dma_start(pos2_t[:], pos2)
+
+        make_identity(nc, ident[:])
+
+        xgw, xgs = {}, {}
+        for pr in range(E // 2):
+            gw = keep.tile([P, 2 * C], U32, name="xgw%d" % pr, align_bytes=64)
+            gs = keep.tile([P, 2 * C], U8, name="xgs%d" % pr, align_bytes=64)
+            cols = offs_t[:, pr * 2 * C // PER_COL : (pr + 1) * 2 * C // PER_COL]
+            nc.vector.tensor_copy(gw[:], xw[:].indirect(cols))
+            nc.vector.tensor_copy(gs[:], xs[:, 0, :].indirect(cols))
+            for u in range(2):
+                xgw[2 * pr + u] = gw[:, u * C : (u + 1) * C]
+                xgs[2 * pr + u] = gs[:, u * C : (u + 1) * C]
+
+        hb = {}
+
+        def first_layer(e):
+            hp = hpool.tile([P, H], F32, name="hp")
+            nc.tensor.matmul_mx(
+                out=hp[:], lhsT=xgw[e].bitcast(FP8X4), lhsT_scale=xgs[e],
+                rhs=waw[e].bitcast(FP4X4), rhs_scale=was[:, e, :], start=True, stop=True,
+            )
+            hb[e] = keep.tile([P, H], BF16, name="hb%d" % e, align_bytes=64)
+            nc.scalar.activation(
+                hb[e][:].rearrange("s (u p d) -> s u p d", u=2, d=2),
+                hp[:].rearrange("s (p u d) -> s u p d", u=2, d=2),
+                RELU,
+            )
+
+        hin = {}
+
+        def turn(grp, eng):
+            n = len(grp)
+            tp = tpool.tile([P, 2, 2, C], F32, name="tp")
+            for x, e in enumerate(grp):
+                words = hb[e][:].bitcast(F32)
+                for u in range(2):
+                    nc.tensor.transpose(tp[:, x, u, :], words[:, u * P : (u + 1) * P], ident[:])
+            hin[grp] = keep.tile([P, n * C * 4], BF16, name="hin%d" % grp[0], align_bytes=64)
+            dst = hin[grp][:].bitcast(F32).rearrange("p (x s u) -> p x s u", x=n, u=2)
+            src = tp[:, 0:n, :, :].rearrange("p x u s -> p x s u")
+            if eng == "scalar":
+                nc.scalar.copy(dst, src)
+            else:
+                nc.vector.tensor_copy(dst, src)
+
+        banks = [ypool.tile([P, 4, C], F32, name="yb%d" % b) for b in range(4)]
+
+        def y_place(e, half):
+            if e < 4:
+                return banks[half][:, e, :]
+            return banks[e // 2][:, 2 * half + e % 2, :]
+
+        def second_layer(grp):
+            n = len(grp)
+            hq = keep.tile([P, n * C], U32, name="hq%d" % grp[0], align_bytes=64)
+            hs = keep.tile([P, n * C], U8, name="hs%d" % grp[0], align_bytes=64)
+            nc.vector.quantize_mx(out=hq[:].bitcast(FP8X4), scales=hs[:], in_=hin[grp][:])
+            for x, e in enumerate(grp):
+                for half in range(2):
+                    nc.tensor.matmul_mx(
+                        out=y_place(e, half),
+                        lhsT=wbw[:, e, 2 * P * half : 2 * P * (half + 1)].bitcast(FP4X4),
+                        lhsT_scale=wbs[:, e, P * half : P * (half + 1)],
+                        rhs=hq[:, x * C : (x + 1) * C].bitcast(FP8X4),
+                        rhs_scale=hs[:, x * C : (x + 1) * C],
+                        start=True, stop=True,
+                    )
+
+        ys = [keep.tile([P, S], F32, name="ys%d" % half) for half in range(2)]
+
+        def y_out(bank, half):
+            if bank < 2:
+                nc.scalar.copy(ys[half][:, 0 : 4 * C], banks[bank][:].rearrange("p x s -> p (x s)"))
+            else:
+                nc.scalar.copy(
+                    ys[half][:, 2 * bank * C : (2 * bank + 2) * C],
+                    banks[bank][:, 2 * half : 2 * half + 2, :].rearrange("p x s -> p (x s)"),
+                )
+
+        for e in range(E):
+            first_layer(e)
+        turn((0, 1), "vector")
+        turn((2, 3), "vector")
+        second_layer((0, 1))
+        turn((4, 5), "scalar")
+        second_layer((2, 3))
+        turn((6,), "scalar")
+        turn((7,), "scalar")
+        second_layer((4, 5))
+        y_out(0, 0)
+        second_layer((6,))
+        second_layer((7,))
+        y_out(2, 0)
+        y_out(3, 0)
+        base = []
+        for half in range(2):
+            bp = hpool.tile([P, T], F32, name="hp")
+            nc.tensor.matmul_mx(
+                out=bp[:], lhsT=ww[:, P * half : P * (half + 1)].bitcast(FP8X4), lhsT_scale=ws[:, 0, P * half : P * (half + 1)],
+                rhs=xw[:].bitcast(FP8X4), rhs_scale=xs[:, 0, :], start=True, stop=True,
+            )
+            base.append(bp)
+        y_out(1, 1)
+        y_out(2, 1)
+        y_out(3, 1)
+
+        a = [keep.tile([P, T], F32, name="a%d" % half) for half in range(2)]
+        b = [keep.tile([P, T], F32, name="b%d" % half) for half in range(2)]
+        s = [keep.tile([P, T], F32, name="s%d" % half) for half in range(2)]
+
+        def fetch(dst, half, r, t0, t1):
+            lst = (pos1_t, pos2_t)[r]
+            nc.vector.tensor_tensor(
+                dst[half][:, t0:t1], ys[half][:].indirect(lst[:, t0 // PER_COL : t1 // PER_COL]), gate_t[:, r, t0:t1], MULT
+            )
+
+        def finish(half, t0, t1):
+            o = keep.tile([P, t1 - t0], F32, name="o%d_%d" % (half, t0))
+            nc.vector.tensor_tensor(o[:], s[half][:, t0:t1], b[half][:, t0:t1], ADD)
+            nc.sync.dma_start(out=out[P * half : P * (half + 1), t0:t1], in_=o[:])
+
+        fetch(a, 0, 0, 0, T)
+        fetch(b, 0, 1, 0, T)
+        nc.vector.tensor_tensor(s[0][:], base[0][:], a[0][:], ADD)
+        fetch(a, 1, 0, 0, T)
+        finish(0, 0, T)
+        nc.vector.tensor_tensor(s[1][:], base[1][:], a[1][:], ADD)
+        fetch(b, 1, 1, 0, T // 2)
+        fetch(b, 1, 1, T // 2, T)
+        finish(1, 0, T // 2)
+        finish(1, T // 2, T)

@@ -23,11 +23,20 @@ P = 128
 PER_COL = 16
 
 
-def load_scale_rows(nc, plane, rows):
+def load_scale_rows(queues, plane, rows):
+    for r in range(4):
+        queues[r].dma_start(
+            out=plane[r:P:32, :, :].bitcast(I32),
+            in_=rows[:, r:16:4, :].rearrange("g q c -> q g c").bitcast(I32),
+        )
+
+
+def fill_scale_plane(queues, plane, rows):
+    words = rows.bitcast(I32)
     for q in range(4):
-        nc.sync.dma_start(
-            out=plane[32 * q : 32 * q + 4, :, :].bitcast(I32),
-            in_=rows[:, 4 * q : 4 * q + 4, :].rearrange("g r c -> r g c").bitcast(I32),
+        queues[q].dma_start(
+            out=plane[32 * q : 32 * q + 32, 0, :].bitcast(I32),
+            in_=words[4 * q : 4 * q + 4, :].unsqueeze(0).broadcast_to([8, 4, words.shape[1]]),
         )
 
 
@@ -37,9 +46,10 @@ def tile_moe_adp_relu_kernel(
     nc = tc.nc
     with ExitStack() as ctx:
         keep = ctx.enter_context(tc.tile_pool(name="keep", bufs=1))
-        hpool = ctx.enter_context(tc.psum_pool(name="hpool", bufs=2))
-        tpool = ctx.enter_context(tc.psum_pool(name="tpool", bufs=2))
-        ypool = ctx.enter_context(tc.psum_pool(name="ypool", bufs=1))
+        psum = ctx.enter_context(tc.psum_pool(name="psum", bufs=1))
+
+        def bank(b, shape, name):
+            return psum.tile(shape, F32, name=name, tag="bank%d" % b)
 
         offs_t = keep.tile([P, S // PER_COL], U16, name="offs_t")
         pos1_t = keep.tile([P, T // PER_COL], U16, name="pos1_t")
@@ -48,12 +58,12 @@ def tile_moe_adp_relu_kernel(
         xs = keep.tile([P, 1, T], U8, name="xs", align_bytes=64)
         ww = keep.tile([P, N], U32, name="ww", align_bytes=64)
         ws = keep.tile([P, 1, N], U8, name="ws", align_bytes=64)
-        was = keep.tile([P, E, H], U8, name="was", align_bytes=64)
+        was_t = [keep.tile([P, 4, H], U8, name="was%d" % i, align_bytes=64) for i in range(2)]
         wbs = keep.tile([P, E, N], U8, name="wbs", align_bytes=64)
         wbw = keep.tile([P, E, 2 * N], U8, name="wbw", align_bytes=64)
         gate_t = keep.tile([P, 2, T], F32, name="gate_t")
         ident = keep.tile([P, P], F32, name="ident")
-        wa_cuts = [(0, 2), (2, 4), (4, 8)]
+        wa_cuts = [(0, 2), (2, 4), (4, 6), (6, 8)]
         waw_t = [keep.tile([P, b - a, 2 * H], U8, name="waw%d" % a, align_bytes=64) for a, b in wa_cuts]
         waw = {}
         for (a, b), tl in zip(wa_cuts, waw_t):
@@ -64,57 +74,67 @@ def tile_moe_adp_relu_kernel(
             a, b = wa_cuts[i]
             eng.dma_start(out=waw_t[i][:].bitcast(I32), in_=wa_words[a:b, 0].rearrange("e p c -> p e c").bitcast(I32))
 
-        for plane in (xs, was, wbs, ws):
-            nc.vector.memset(plane[:].bitcast(I32), 0)
+        warm = keep.tile([P, 2], F32, name="warm")
+        nc.vector.memset(warm[:, 0:1], 0.0)
+        for plane in was_t:
+            words = plane[:].rearrange("p e c -> p (e c)").bitcast(I32)
+            nc.vector.memset(words[:, 0:320], 0)
+            nc.gpsimd.memset(words[:, 320:512], 0)
+        nc.vector.memset(wbs[:].bitcast(I32), 0)
+        make_identity(nc, ident[:])
 
-        nc.sync.dma_start(offs_t[:], offs)
+        both = (nc.sync, nc.scalar, nc.sync, nc.scalar)
+        fill_scale_plane(both, xs, x_scales[0])
         nc.scalar.dma_start(out=xw[:].bitcast(I32), in_=x_words[0].rearrange("p t d -> p (t d)").bitcast(I32))
-        load_scale_rows(nc, xs, x_scales)
-        load_wa(0, nc.scalar)
-        load_scale_rows(nc, was, wa_scales[:, 0])
+        nc.scalar.activation(warm[:, 1:2], warm[:, 0:1], RELU)
+        nc.sync.dma_start(offs_t[:], offs)
+        load_wa(0, nc.sync)
+        load_scale_rows(both, was_t[0], wa_scales[0:4, 0])
         load_wa(1, nc.sync)
         load_wa(2, nc.sync)
+        load_scale_rows(both, was_t[1], wa_scales[4:8, 0])
+        load_wa(3, nc.sync)
         nc.sync.dma_start(out=wbw[:].bitcast(I32), in_=wb_words[:, 0].rearrange("e p c -> p e c").bitcast(I32))
-        load_scale_rows(nc, wbs, wb_scales[:, 0])
-        nc.sync.dma_start(out=ww[:].bitcast(I32), in_=w_words[0].rearrange("p n d -> p (n d)").bitcast(I32))
-        load_scale_rows(nc, ws, w_scales)
+        load_scale_rows((nc.sync,) * 4, wbs, wb_scales[:, 0])
         nc.sync.dma_start(out=gate_t[:], in_=gate.rearrange("r p t -> p r t"))
         nc.sync.dma_start(pos1_t[:], pos1)
         nc.sync.dma_start(pos2_t[:], pos2)
-
-        make_identity(nc, ident[:])
+        nc.sync.dma_start(out=ww[:].bitcast(I32), in_=w_words[0].rearrange("p n d -> p (n d)").bitcast(I32))
+        fill_scale_plane((nc.sync,) * 4, ws, w_scales[0])
 
         xgw, xgs = {}, {}
-        for pr in range(E // 2):
-            gw = keep.tile([P, 2 * C], U32, name="xgw%d" % pr, align_bytes=64)
-            gs = keep.tile([P, 2 * C], U8, name="xgs%d" % pr, align_bytes=64)
-            cols = offs_t[:, pr * 2 * C // PER_COL : (pr + 1) * 2 * C // PER_COL]
+        for grp in [(0,), (1, 2), (3, 4), (5, 6), (7,)]:
+            n = len(grp)
+            gw = keep.tile([P, n * C], U32, name="xgw%d" % grp[0], align_bytes=64)
+            gs = keep.tile([P, n * C], U8, name="xgs%d" % grp[0], align_bytes=64)
+            cols = offs_t[:, grp[0] * C // PER_COL : (grp[0] + n) * C // PER_COL]
             nc.vector.tensor_copy(gw[:], xw[:].indirect(cols))
             nc.vector.tensor_copy(gs[:], xs[:, 0, :].indirect(cols))
-            for u in range(2):
-                xgw[2 * pr + u] = gw[:, u * C : (u + 1) * C]
-                xgs[2 * pr + u] = gs[:, u * C : (u + 1) * C]
+            for u, e in enumerate(grp):
+                xgw[e] = gw[:, u * C : (u + 1) * C]
+                xgs[e] = gs[:, u * C : (u + 1) * C]
 
         hb = {}
 
-        def first_layer(e):
-            hp = hpool.tile([P, H], F32, name="hp")
+        def first_layer(e, eng):
+            hp = bank(e % 4, [P, H], "hp%d" % e)
             nc.tensor.matmul_mx(
                 out=hp[:], lhsT=xgw[e].bitcast(FP8X4), lhsT_scale=xgs[e],
-                rhs=waw[e].bitcast(FP4X4), rhs_scale=was[:, e, :], start=True, stop=True,
+                rhs=waw[e].bitcast(FP4X4), rhs_scale=was_t[e // 4][:, e % 4, :], start=True, stop=True,
             )
             hb[e] = keep.tile([P, H], BF16, name="hb%d" % e, align_bytes=64)
-            nc.scalar.activation(
-                hb[e][:].rearrange("s (u p d) -> s u p d", u=2, d=2),
-                hp[:].rearrange("s (p u d) -> s u p d", u=2, d=2),
-                RELU,
-            )
+            dst = hb[e][:].rearrange("s (u p d) -> s u p d", u=2, d=2)
+            src = hp[:].rearrange("s (p u d) -> s u p d", u=2, d=2)
+            if eng == "scalar":
+                nc.scalar.activation(dst, src, RELU)
+            else:
+                nc.vector.tensor_scalar_max(dst, src, 0.0)
 
         hin = {}
 
-        def turn(grp, eng):
+        def turn(grp, eng, b):
             n = len(grp)
-            tp = tpool.tile([P, 2, 2, C], F32, name="tp")
+            tp = bank(b, [P, 2, 2, C], "tp%d" % grp[0])
             for x, e in enumerate(grp):
                 words = hb[e][:].bitcast(F32)
                 for u in range(2):
@@ -127,66 +147,79 @@ def tile_moe_adp_relu_kernel(
             else:
                 nc.vector.tensor_copy(dst, src)
 
-        banks = [ypool.tile([P, 4, C], F32, name="yb%d" % b) for b in range(4)]
+        hq, hs = {}, {}
 
-        def y_place(e, half):
-            if e < 4:
-                return banks[half][:, e, :]
-            return banks[e // 2][:, 2 * half + e % 2, :]
-
-        def second_layer(grp):
+        def quantize(grp):
             n = len(grp)
-            hq = keep.tile([P, n * C], U32, name="hq%d" % grp[0], align_bytes=64)
-            hs = keep.tile([P, n * C], U8, name="hs%d" % grp[0], align_bytes=64)
-            nc.vector.quantize_mx(out=hq[:].bitcast(FP8X4), scales=hs[:], in_=hin[grp][:])
+            codes = keep.tile([P, n * C], U32, name="hq%d" % grp[0], align_bytes=64)
+            scales = keep.tile([P, n * C], U8, name="hs%d" % grp[0], align_bytes=64)
+            nc.vector.quantize_mx(out=codes[:].bitcast(FP8X4), scales=scales[:], in_=hin[grp][:])
             for x, e in enumerate(grp):
-                for half in range(2):
-                    nc.tensor.matmul_mx(
-                        out=y_place(e, half),
-                        lhsT=wbw[:, e, 2 * P * half : 2 * P * (half + 1)].bitcast(FP4X4),
-                        lhsT_scale=wbs[:, e, P * half : P * (half + 1)],
-                        rhs=hq[:, x * C : (x + 1) * C].bitcast(FP8X4),
-                        rhs_scale=hs[:, x * C : (x + 1) * C],
-                        start=True, stop=True,
-                    )
+                hq[e] = codes[:, x * C : (x + 1) * C]
+                hs[e] = scales[:, x * C : (x + 1) * C]
+
+        y_groups = [[((0, 1, 2, 3), 6), ((4, 5, 6), 7), ((7,), 2)], [((0, 1, 2, 3), 1), ((4, 5, 6, 7), 3)]]
+        y_tiles = {}
+
+        def second_layer(grp, half):
+            for e in grp:
+                members, b = [g for g in y_groups[half] if e in g[0]][0]
+                if (members, half) not in y_tiles:
+                    y_tiles[(members, half)] = bank(b, [P, len(members) * C], "y%d_%d" % (half, members[0]))
+                x = e - members[0]
+                nc.tensor.matmul_mx(
+                    out=y_tiles[(members, half)][:, x * C : (x + 1) * C],
+                    lhsT=wbw[:, e, 2 * P * half : 2 * P * (half + 1)].bitcast(FP4X4),
+                    lhsT_scale=wbs[:, e, P * half : P * (half + 1)],
+                    rhs=hq[e].bitcast(FP8X4), rhs_scale=hs[e], start=True, stop=True,
+                )
 
         ys = [keep.tile([P, S], F32, name="ys%d" % half) for half in range(2)]
 
-        def y_out(bank, half):
-            if bank < 2:
-                nc.scalar.copy(ys[half][:, 0 : 4 * C], banks[bank][:].rearrange("p x s -> p (x s)"))
+        def y_out(members, half, eng):
+            dst = ys[half][:, members[0] * C : (members[-1] + 1) * C]
+            if eng == "scalar":
+                nc.scalar.copy(dst, y_tiles[(members, half)][:])
             else:
-                nc.scalar.copy(
-                    ys[half][:, 2 * bank * C : (2 * bank + 2) * C],
-                    banks[bank][:, 2 * half : 2 * half + 2, :].rearrange("p x s -> p (x s)"),
-                )
+                nc.vector.tensor_copy(dst, y_tiles[(members, half)][:])
 
-        for e in range(E):
-            first_layer(e)
-        turn((0, 1), "vector")
-        turn((2, 3), "vector")
-        second_layer((0, 1))
-        turn((4, 5), "scalar")
-        second_layer((2, 3))
-        turn((6,), "scalar")
-        turn((7,), "scalar")
-        second_layer((4, 5))
-        y_out(0, 0)
-        second_layer((6,))
-        second_layer((7,))
-        y_out(2, 0)
-        y_out(3, 0)
-        base = []
-        for half in range(2):
-            bp = hpool.tile([P, T], F32, name="hp")
+        def quantize_and_multiply(grp):
+            quantize(grp)
+            second_layer(grp, 0)
+
+        base = {}
+
+        def frozen_layer(half, b):
+            base[half] = bank(b, [P, T], "base%d" % half)
             nc.tensor.matmul_mx(
-                out=bp[:], lhsT=ww[:, P * half : P * (half + 1)].bitcast(FP8X4), lhsT_scale=ws[:, 0, P * half : P * (half + 1)],
+                out=base[half][:], lhsT=ww[:, P * half : P * (half + 1)].bitcast(FP8X4), lhsT_scale=ws[:, 0, P * half : P * (half + 1)],
                 rhs=xw[:].bitcast(FP8X4), rhs_scale=xs[:, 0, :], start=True, stop=True,
             )
-            base.append(bp)
-        y_out(1, 1)
-        y_out(2, 1)
-        y_out(3, 1)
+
+        for e in range(4):
+            first_layer(e, "scalar")
+        turn((0, 1), "scalar", 4)
+        first_layer(4, "vector")
+        first_layer(5, "vector")
+        first_layer(6, "scalar")
+        first_layer(7, "scalar")
+        quantize_and_multiply((0, 1))
+        turn((2, 3), "vector", 5)
+        turn((4, 5), "scalar", 4)
+        quantize_and_multiply((2, 3))
+        turn((6,), "scalar", 5)
+        turn((7,), "scalar", 0)
+        quantize_and_multiply((4, 5))
+        quantize_and_multiply((6,))
+        quantize_and_multiply((7,))
+        y_out((0, 1, 2, 3), 0, "scalar")
+        y_out((4, 5, 6), 0, "vector")
+        y_out((7,), 0, "scalar")
+        second_layer(range(E), 1)
+        frozen_layer(0, 4)
+        frozen_layer(1, 5)
+        y_out((0, 1, 2, 3), 1, "scalar")
+        y_out((4, 5, 6, 7), 1, "scalar")
 
         a = [keep.tile([P, T], F32, name="a%d" % half) for half in range(2)]
         b = [keep.tile([P, T], F32, name="b%d" % half) for half in range(2)]
@@ -203,13 +236,32 @@ def tile_moe_adp_relu_kernel(
             nc.vector.tensor_tensor(o[:], s[half][:, t0:t1], b[half][:, t0:t1], ADD)
             nc.sync.dma_start(out=out[P * half : P * (half + 1), t0:t1], in_=o[:])
 
-        fetch(a, 0, 0, 0, T)
-        fetch(b, 0, 1, 0, T)
-        nc.vector.tensor_tensor(s[0][:], base[0][:], a[0][:], ADD)
+        base_sb = keep.tile([P, T], F32, name="base_sb")
+        nc.scalar.copy(base_sb[:], base[0][:])
+
+        def add_on_tensor(t0, b1, b2):
+            p1 = bank(b1, [P, 2, P], "sum_t%d" % t0)
+            for j in range(2):
+                cols = slice(t0 + j * P, t0 + (j + 1) * P)
+                for i, src in enumerate((base_sb, a[0], b[0])):
+                    nc.tensor.matmul(p1[:, j, :], lhsT=src[:, cols], rhs=ident[:], is_transpose=True, start=(i == 0), stop=(i == 2))
+            m = keep.tile([P, 2, P], F32, name="m%d" % t0)
+            nc.scalar.copy(m[:], p1[:])
+            p2 = bank(b2, [P, 2, P], "sum%d" % t0)
+            for j in range(2):
+                nc.tensor.transpose(p2[:, j, :], m[:, j, :], ident[:])
+            o = keep.tile([P, 2 * P], F32, name="o0_%d" % t0)
+            nc.scalar.copy(o[:], p2[:].rearrange("p j t -> p (j t)"))
+            nc.sync.dma_start(out=out[0:P, t0 : t0 + 2 * P], in_=o[:])
+
+        for t0 in (0, T // 2):
+            fetch(a, 0, 0, t0, t0 + T // 2)
+            fetch(b, 0, 1, t0, t0 + T // 2)
         fetch(a, 1, 0, 0, T)
-        finish(0, 0, T)
-        nc.vector.tensor_tensor(s[1][:], base[1][:], a[1][:], ADD)
         fetch(b, 1, 1, 0, T // 2)
+        nc.vector.tensor_tensor(s[1][:], base[1][:], a[1][:], ADD)
         fetch(b, 1, 1, T // 2, T)
+        add_on_tensor(0, 6, 2)
+        add_on_tensor(T // 2, 7, 0)
         finish(1, 0, T // 2)
         finish(1, T // 2, T)

@@ -96,14 +96,14 @@ def tile_moe_adp_relu_kernel(
         load_wa(3, nc.sync)
         nc.sync.dma_start(out=wbw[:].bitcast(I32), in_=wb_words[:, 0].rearrange("e p c -> p e c").bitcast(I32))
         load_scale_rows((nc.sync,) * 4, wbs, wb_scales[:, 0])
-        nc.sync.dma_start(out=gate_t[:], in_=gate.rearrange("r p t -> p r t"))
-        nc.sync.dma_start(pos1_t[:], pos1)
-        nc.sync.dma_start(pos2_t[:], pos2)
         nc.sync.dma_start(out=ww[:].bitcast(I32), in_=w_words[0].rearrange("p n d -> p (n d)").bitcast(I32))
         fill_scale_plane((nc.sync,) * 4, ws, w_scales[0])
+        nc.sync.dma_start(pos1_t[:], pos1)
+        nc.sync.dma_start(pos2_t[:], pos2)
+        nc.sync.dma_start(out=gate_t[:], in_=gate.rearrange("r p t -> p r t"))
 
         xgw, xgs = {}, {}
-        for grp in [(0,), (1, 2), (3, 4), (5, 6), (7,)]:
+        for grp in [(0, 1), (2, 3), (4, 5), (6, 7)]:
             n = len(grp)
             gw = keep.tile([P, n * C], U32, name="xgw%d" % grp[0], align_bytes=64)
             gs = keep.tile([P, n * C], U8, name="xgs%d" % grp[0], align_bytes=64)
@@ -196,25 +196,22 @@ def tile_moe_adp_relu_kernel(
                 rhs=xw[:].bitcast(FP8X4), rhs_scale=xs[:, 0, :], start=True, stop=True,
             )
 
-        for e in range(4):
-            first_layer(e, "scalar")
-        turn((0, 1), "scalar", 4)
-        first_layer(4, "vector")
-        first_layer(5, "vector")
-        first_layer(6, "scalar")
-        first_layer(7, "scalar")
+        for e in range(E):
+            first_layer(e, "vector" if e in (4, 5, 7) else "scalar")
+            if e == 3:
+                turn((0, 1), "scalar", 4)
+        turn((2, 3), "scalar", 5)
         quantize_and_multiply((0, 1))
-        turn((2, 3), "vector", 5)
-        turn((4, 5), "scalar", 4)
+        turn((4, 5), "scalar", 0)
         quantize_and_multiply((2, 3))
-        turn((6,), "scalar", 5)
-        turn((7,), "scalar", 0)
+        turn((6,), "scalar", 4)
+        turn((7,), "scalar", 5)
         quantize_and_multiply((4, 5))
         quantize_and_multiply((6,))
         quantize_and_multiply((7,))
         y_out((0, 1, 2, 3), 0, "scalar")
-        y_out((4, 5, 6), 0, "vector")
-        y_out((7,), 0, "scalar")
+        y_out((4, 5, 6), 0, "scalar")
+        y_out((7,), 0, "vector")
         second_layer(range(E), 1)
         frozen_layer(0, 4)
         frozen_layer(1, 5)

@@ -213,7 +213,12 @@ def tile_moe_adp_relu_kernel(
         y_out((4, 5, 6), 0, "scalar")
         y_out((7,), 0, "vector")
         second_layer(range(E), 1)
-        frozen_layer(0, 4)
+        base_t = bank(4, [P, 4, P], "base_t")
+        for j in range(4):
+            nc.tensor.matmul_mx(
+                out=base_t[:, j, :], lhsT=xw[:, j * P : (j + 1) * P].bitcast(FP8X4), lhsT_scale=xs[:, 0, j * P : (j + 1) * P],
+                rhs=ww[:, 0:P].bitcast(FP8X4), rhs_scale=ws[:, 0, 0:P], start=True, stop=True,
+            )
         frozen_layer(1, 5)
         y_out((0, 1, 2, 3), 1, "scalar")
         y_out((4, 5, 6, 7), 1, "scalar")
@@ -233,20 +238,21 @@ def tile_moe_adp_relu_kernel(
             nc.vector.tensor_tensor(o[:], s[half][:, t0:t1], b[half][:, t0:t1], ADD)
             nc.sync.dma_start(out=out[P * half : P * (half + 1), t0:t1], in_=o[:])
 
-        base_sb = keep.tile([P, T], F32, name="base_sb")
-        nc.scalar.copy(base_sb[:], base[0][:])
+        base_sb = keep.tile([P, 4, P], F32, name="base_sb")
+        nc.scalar.copy(base_sb[:], base_t[:])
 
         def add_on_tensor(t0, b1, b2):
             p1 = bank(b1, [P, 2, P], "sum_t%d" % t0)
             for j in range(2):
                 cols = slice(t0 + j * P, t0 + (j + 1) * P)
-                for i, src in enumerate((base_sb, a[0], b[0])):
-                    nc.tensor.matmul(p1[:, j, :], lhsT=src[:, cols], rhs=ident[:], is_transpose=True, start=(i == 0), stop=(i == 2))
+                for i, src in enumerate((a[0], b[0])):
+                    nc.tensor.matmul(p1[:, j, :], lhsT=src[:, cols], rhs=ident[:], is_transpose=True, start=(i == 0), stop=(i == 1))
             m = keep.tile([P, 2, P], F32, name="m%d" % t0)
             nc.scalar.copy(m[:], p1[:])
             p2 = bank(b2, [P, 2, P], "sum%d" % t0)
             for j in range(2):
-                nc.tensor.transpose(p2[:, j, :], m[:, j, :], ident[:])
+                for i, src in enumerate((base_sb[:, t0 // P + j, :], m[:, j, :])):
+                    nc.tensor.matmul(p2[:, j, :], lhsT=src, rhs=ident[:], is_transpose=True, start=(i == 0), stop=(i == 1))
             o = keep.tile([P, 2 * P], F32, name="o0_%d" % t0)
             nc.scalar.copy(o[:], p2[:].rearrange("p j t -> p (j t)"))
             nc.sync.dma_start(out=out[0:P, t0 : t0 + 2 * P], in_=o[:])

@@ -4,8 +4,8 @@ import concourse.mybir as mybir
 from concourse.masks import make_identity
 
 K, T, E, C, H, N = 512, 512, 8, 128, 512, 256
-S = E * C
-FLOPS = 2 * K * N * T + 2 * K * H * S + 2 * H * N * S
+SLOTS = E * C
+FLOPS = 2 * K * N * T + 2 * K * H * SLOTS + 2 * H * N * SLOTS
 
 F32 = mybir.dt.float32
 BF16 = mybir.dt.bfloat16
@@ -20,7 +20,12 @@ ADD = mybir.AluOpType.add
 RELU = mybir.ActivationFunctionType.Relu
 
 P = 128
-PER_COL = 16
+LIST_COLUMN = 16
+PAIRS = [(0, 1), (2, 3), (4, 5), (6, 7)]
+PLANE_ADAPTERS = 4
+VECTOR_ZERO_WORDS = 320
+VECTOR_RELU = (4, 5, 7)
+Y_GROUPS = [[((0, 1, 2, 3), 6), ((4, 5, 6), 7), ((7,), 2)], [((0, 1, 2, 3), 1), ((4, 5, 6, 7), 3)]]
 
 
 def load_scale_rows(queues, plane, rows):
@@ -35,7 +40,7 @@ def fill_scale_plane(queues, plane, rows):
     words = rows.bitcast(I32)
     for q in range(4):
         queues[q].dma_start(
-            out=plane[32 * q : 32 * q + 32, 0, :].bitcast(I32),
+            out=plane[32 * q : 32 * q + 32, :].bitcast(I32),
             in_=words[4 * q : 4 * q + 4, :].unsqueeze(0).broadcast_to([8, 4, words.shape[1]]),
         )
 
@@ -48,223 +53,223 @@ def tile_moe_adp_relu_kernel(
         keep = ctx.enter_context(tc.tile_pool(name="keep", bufs=1))
         psum = ctx.enter_context(tc.psum_pool(name="psum", bufs=1))
 
-        def bank(b, shape, name):
-            return psum.tile(shape, F32, name=name, tag="bank%d" % b)
+        def bank(number, shape, name):
+            return psum.tile(shape, F32, name=name, tag="bank%d" % number)
 
-        offs_t = keep.tile([P, S // PER_COL], U16, name="offs_t")
-        pos1_t = keep.tile([P, T // PER_COL], U16, name="pos1_t")
-        pos2_t = keep.tile([P, T // PER_COL], U16, name="pos2_t")
-        xw = keep.tile([P, T], U32, name="xw", align_bytes=64)
-        xs = keep.tile([P, 1, T], U8, name="xs", align_bytes=64)
-        ww = keep.tile([P, N], U32, name="ww", align_bytes=64)
-        ws = keep.tile([P, 1, N], U8, name="ws", align_bytes=64)
-        was_t = [keep.tile([P, 4, H], U8, name="was%d" % i, align_bytes=64) for i in range(2)]
-        wbs = keep.tile([P, E, N], U8, name="wbs", align_bytes=64)
-        wbw = keep.tile([P, E, 2 * N], U8, name="wbw", align_bytes=64)
+        offs_t = keep.tile([P, SLOTS // LIST_COLUMN], U16, name="offs_t")
+        pos_t = [keep.tile([P, T // LIST_COLUMN], U16, name="pos%d_t" % r) for r in (1, 2)]
+        x_w = keep.tile([P, T], U32, name="x_w", align_bytes=64)
+        x_plane = keep.tile([P, T], U8, name="x_plane", align_bytes=64)
+        w_w = keep.tile([P, N], U32, name="w_w", align_bytes=64)
+        w_plane = keep.tile([P, N], U8, name="w_plane", align_bytes=64)
+        wa_planes = [
+            keep.tile([P, PLANE_ADAPTERS, H], U8, name="wa_plane%d" % g, align_bytes=64) for g in range(E // PLANE_ADAPTERS)
+        ]
+        wb_plane = keep.tile([P, E, N], U8, name="wb_plane", align_bytes=64)
+        wb_w = keep.tile([P, E, 2 * N], U8, name="wb_w", align_bytes=64)
         gate_t = keep.tile([P, 2, T], F32, name="gate_t")
         ident = keep.tile([P, P], F32, name="ident")
-        wa_cuts = [(0, 2), (2, 4), (4, 6), (6, 8)]
-        waw_t = [keep.tile([P, b - a, 2 * H], U8, name="waw%d" % a, align_bytes=64) for a, b in wa_cuts]
-        waw = {}
-        for (a, b), tl in zip(wa_cuts, waw_t):
-            for e in range(a, b):
-                waw[e] = tl[:, e - a, :]
+        wa_w = [keep.tile([P, 2, 2 * H], U8, name="wa_w%d" % pair[0], align_bytes=64) for pair in PAIRS]
 
-        def load_wa(i, eng):
-            a, b = wa_cuts[i]
-            eng.dma_start(out=waw_t[i][:].bitcast(I32), in_=wa_words[a:b, 0].rearrange("e p c -> p e c").bitcast(I32))
+        def load_wa_words(pair):
+            rows = wa_words[2 * pair : 2 * pair + 2, 0].rearrange("e p c -> p e c")
+            nc.sync.dma_start(out=wa_w[pair][:].bitcast(I32), in_=rows.bitcast(I32))
 
-        warm = keep.tile([P, 2], F32, name="warm")
-        nc.vector.memset(warm[:, 0:1], 0.0)
-        for plane in was_t:
+        def load_wa_plane(g):
+            load_scale_rows(both_queues, wa_planes[g], wa_scales[PLANE_ADAPTERS * g : PLANE_ADAPTERS * (g + 1), 0])
+
+        for plane in wa_planes:
             words = plane[:].rearrange("p e c -> p (e c)").bitcast(I32)
-            nc.vector.memset(words[:, 0:320], 0)
-            nc.gpsimd.memset(words[:, 320:512], 0)
-        nc.vector.memset(wbs[:].bitcast(I32), 0)
+            nc.vector.memset(words[:, 0:VECTOR_ZERO_WORDS], 0)
+            nc.gpsimd.memset(words[:, VECTOR_ZERO_WORDS:], 0)
+        nc.vector.memset(wb_plane[:].bitcast(I32), 0)
         make_identity(nc, ident[:])
 
-        both = (nc.sync, nc.scalar, nc.sync, nc.scalar)
-        fill_scale_plane(both, xs, x_scales[0])
-        nc.scalar.dma_start(out=xw[:].bitcast(I32), in_=x_words[0].rearrange("p t d -> p (t d)").bitcast(I32))
-        nc.scalar.activation(warm[:, 1:2], warm[:, 0:1], RELU)
+        both_queues = (nc.sync, nc.scalar, nc.sync, nc.scalar)
+        sync_queue = (nc.sync,) * 4
+        fill_scale_plane(both_queues, x_plane, x_scales[0])
+        nc.scalar.dma_start(out=x_w[:].bitcast(I32), in_=x_words[0].rearrange("p t d -> p (t d)").bitcast(I32))
         nc.sync.dma_start(offs_t[:], offs)
-        load_wa(0, nc.sync)
-        load_scale_rows(both, was_t[0], wa_scales[0:4, 0])
-        load_wa(1, nc.sync)
-        load_wa(2, nc.sync)
-        load_scale_rows(both, was_t[1], wa_scales[4:8, 0])
-        load_wa(3, nc.sync)
-        nc.sync.dma_start(out=wbw[:].bitcast(I32), in_=wb_words[:, 0].rearrange("e p c -> p e c").bitcast(I32))
-        load_scale_rows((nc.sync,) * 4, wbs, wb_scales[:, 0])
-        nc.sync.dma_start(out=ww[:].bitcast(I32), in_=w_words[0].rearrange("p n d -> p (n d)").bitcast(I32))
-        fill_scale_plane((nc.sync,) * 4, ws, w_scales[0])
-        nc.sync.dma_start(pos1_t[:], pos1)
-        nc.sync.dma_start(pos2_t[:], pos2)
+        load_wa_words(0)
+        load_wa_plane(0)
+        load_wa_words(1)
+        load_wa_words(2)
+        load_wa_plane(1)
+        load_wa_words(3)
+        nc.sync.dma_start(out=wb_w[:].bitcast(I32), in_=wb_words[:, 0].rearrange("e p c -> p e c").bitcast(I32))
+        load_scale_rows(sync_queue, wb_plane, wb_scales[:, 0])
+        nc.sync.dma_start(out=w_w[:].bitcast(I32), in_=w_words[0].rearrange("p n d -> p (n d)").bitcast(I32))
+        fill_scale_plane(sync_queue, w_plane, w_scales[0])
+        nc.sync.dma_start(pos_t[0][:], pos1)
+        nc.sync.dma_start(pos_t[1][:], pos2)
         nc.sync.dma_start(out=gate_t[:], in_=gate.rearrange("r p t -> p r t"))
 
-        xgw, xgs = {}, {}
-        for grp in [(0, 1), (2, 3), (4, 5), (6, 7)]:
-            n = len(grp)
-            gw = keep.tile([P, n * C], U32, name="xgw%d" % grp[0], align_bytes=64)
-            gs = keep.tile([P, n * C], U8, name="xgs%d" % grp[0], align_bytes=64)
-            cols = offs_t[:, grp[0] * C // PER_COL : (grp[0] + n) * C // PER_COL]
-            nc.vector.tensor_copy(gw[:], xw[:].indirect(cols))
-            nc.vector.tensor_copy(gs[:], xs[:, 0, :].indirect(cols))
-            for u, e in enumerate(grp):
-                xgw[e] = gw[:, u * C : (u + 1) * C]
-                xgs[e] = gs[:, u * C : (u + 1) * C]
+        slot_w, slot_plane = {}, {}
+        for pair in PAIRS:
+            words = keep.tile([P, 2 * C], U32, name="slot_w%d" % pair[0], align_bytes=64)
+            plane = keep.tile([P, 2 * C], U8, name="slot_plane%d" % pair[0], align_bytes=64)
+            entries = offs_t[:, pair[0] * C // LIST_COLUMN : (pair[0] + 2) * C // LIST_COLUMN]
+            nc.vector.tensor_copy(words[:], x_w[:].indirect(entries))
+            nc.vector.tensor_copy(plane[:], x_plane[:].indirect(entries))
+            for x, e in enumerate(pair):
+                slot_w[e] = words[:, x * C : (x + 1) * C]
+                slot_plane[e] = plane[:, x * C : (x + 1) * C]
 
-        hb = {}
+        h_rows = {}
 
-        def first_layer(e, eng):
-            hp = bank(e % 4, [P, H], "hp%d" % e)
+        def first_layer(e):
+            sums = bank(e % 4, [P, H], "h_sums%d" % e)
             nc.tensor.matmul_mx(
-                out=hp[:], lhsT=xgw[e].bitcast(FP8X4), lhsT_scale=xgs[e],
-                rhs=waw[e].bitcast(FP4X4), rhs_scale=was_t[e // 4][:, e % 4, :], start=True, stop=True,
+                out=sums[:],
+                lhsT=slot_w[e].bitcast(FP8X4),
+                lhsT_scale=slot_plane[e],
+                rhs=wa_w[e // 2][:, e % 2, :].bitcast(FP4X4),
+                rhs_scale=wa_planes[e // PLANE_ADAPTERS][:, e % PLANE_ADAPTERS, :],
+                start=True,
+                stop=True,
             )
-            hb[e] = keep.tile([P, H], BF16, name="hb%d" % e, align_bytes=64)
-            dst = hb[e][:].rearrange("s (u p d) -> s u p d", u=2, d=2)
-            src = hp[:].rearrange("s (p u d) -> s u p d", u=2, d=2)
-            if eng == "scalar":
-                nc.scalar.activation(dst, src, RELU)
-            else:
+            h_rows[e] = keep.tile([P, H], BF16, name="h_rows%d" % e, align_bytes=64)
+            dst = h_rows[e][:].rearrange("s (u p d) -> s u p d", u=2, d=2)
+            src = sums[:].rearrange("s (p u d) -> s u p d", u=2, d=2)
+            if e in VECTOR_RELU:
                 nc.vector.tensor_scalar_max(dst, src, 0.0)
-
-        hin = {}
-
-        def turn(grp, eng, b):
-            n = len(grp)
-            tp = bank(b, [P, 2, 2, C], "tp%d" % grp[0])
-            for x, e in enumerate(grp):
-                words = hb[e][:].bitcast(F32)
-                for u in range(2):
-                    nc.tensor.transpose(tp[:, x, u, :], words[:, u * P : (u + 1) * P], ident[:])
-            hin[grp] = keep.tile([P, n * C * 4], BF16, name="hin%d" % grp[0], align_bytes=64)
-            dst = hin[grp][:].bitcast(F32).rearrange("p (x s u) -> p x s u", x=n, u=2)
-            src = tp[:, 0:n, :, :].rearrange("p x u s -> p x s u")
-            if eng == "scalar":
-                nc.scalar.copy(dst, src)
             else:
-                nc.vector.tensor_copy(dst, src)
+                nc.scalar.activation(dst, src, RELU)
 
-        hq, hs = {}, {}
+        h_turned = {}
 
-        def quantize(grp):
-            n = len(grp)
-            codes = keep.tile([P, n * C], U32, name="hq%d" % grp[0], align_bytes=64)
-            scales = keep.tile([P, n * C], U8, name="hs%d" % grp[0], align_bytes=64)
-            nc.vector.quantize_mx(out=codes[:].bitcast(FP8X4), scales=scales[:], in_=hin[grp][:])
-            for x, e in enumerate(grp):
-                hq[e] = codes[:, x * C : (x + 1) * C]
-                hs[e] = scales[:, x * C : (x + 1) * C]
+        def turn(group, number):
+            count = len(group)
+            pairs = bank(number, [P, 2, 2, C], "h_pairs%d" % group[0])
+            for x, e in enumerate(group):
+                words = h_rows[e][:].bitcast(F32)
+                for u in range(2):
+                    nc.tensor.transpose(pairs[:, x, u, :], words[:, u * P : (u + 1) * P], ident[:])
+            h_turned[group] = keep.tile([P, count * C * 4], BF16, name="h_turned%d" % group[0], align_bytes=64)
+            nc.scalar.copy(
+                h_turned[group][:].bitcast(F32).rearrange("p (x s u) -> p x s u", x=count, u=2),
+                pairs[:, 0:count, :, :].rearrange("p x u s -> p x s u"),
+            )
 
-        y_groups = [[((0, 1, 2, 3), 6), ((4, 5, 6), 7), ((7,), 2)], [((0, 1, 2, 3), 1), ((4, 5, 6, 7), 3)]]
-        y_tiles = {}
+        h_w, h_plane, y_sums = {}, {}, {}
 
-        def second_layer(grp, half):
-            for e in grp:
-                members, b = [g for g in y_groups[half] if e in g[0]][0]
-                if (members, half) not in y_tiles:
-                    y_tiles[(members, half)] = bank(b, [P, len(members) * C], "y%d_%d" % (half, members[0]))
+        def second_layer(adapters, half):
+            for e in adapters:
+                members, number = [g for g in Y_GROUPS[half] if e in g[0]][0]
+                if (members, half) not in y_sums:
+                    y_sums[(members, half)] = bank(number, [P, len(members) * C], "y_sums%d_%d" % (half, members[0]))
                 x = e - members[0]
                 nc.tensor.matmul_mx(
-                    out=y_tiles[(members, half)][:, x * C : (x + 1) * C],
-                    lhsT=wbw[:, e, 2 * P * half : 2 * P * (half + 1)].bitcast(FP4X4),
-                    lhsT_scale=wbs[:, e, P * half : P * (half + 1)],
-                    rhs=hq[e].bitcast(FP8X4), rhs_scale=hs[e], start=True, stop=True,
+                    out=y_sums[(members, half)][:, x * C : (x + 1) * C],
+                    lhsT=wb_w[:, e, 2 * P * half : 2 * P * (half + 1)].bitcast(FP4X4),
+                    lhsT_scale=wb_plane[:, e, P * half : P * (half + 1)],
+                    rhs=h_w[e].bitcast(FP8X4),
+                    rhs_scale=h_plane[e],
+                    start=True,
+                    stop=True,
                 )
 
-        ys = [keep.tile([P, S], F32, name="ys%d" % half) for half in range(2)]
+        def quantize_and_multiply(group):
+            words = keep.tile([P, len(group) * C], U32, name="h_w%d" % group[0], align_bytes=64)
+            plane = keep.tile([P, len(group) * C], U8, name="h_plane%d" % group[0], align_bytes=64)
+            nc.vector.quantize_mx(out=words[:].bitcast(FP8X4), scales=plane[:], in_=h_turned[group][:])
+            for x, e in enumerate(group):
+                h_w[e] = words[:, x * C : (x + 1) * C]
+                h_plane[e] = plane[:, x * C : (x + 1) * C]
+            second_layer(group, 0)
 
-        def y_out(members, half, eng):
-            dst = ys[half][:, members[0] * C : (members[-1] + 1) * C]
-            if eng == "scalar":
-                nc.scalar.copy(dst, y_tiles[(members, half)][:])
-            else:
-                nc.vector.tensor_copy(dst, y_tiles[(members, half)][:])
+        y = [keep.tile([P, SLOTS], F32, name="y%d" % half) for half in range(2)]
 
-        def quantize_and_multiply(grp):
-            quantize(grp)
-            second_layer(grp, 0)
+        def y_out(half, index, copy):
+            members = Y_GROUPS[half][index][0]
+            copy(y[half][:, members[0] * C : (members[-1] + 1) * C], y_sums[(members, half)][:])
 
-        base = {}
-
-        def frozen_layer(half, b):
-            base[half] = bank(b, [P, T], "base%d" % half)
-            nc.tensor.matmul_mx(
-                out=base[half][:], lhsT=ww[:, P * half : P * (half + 1)].bitcast(FP8X4), lhsT_scale=ws[:, 0, P * half : P * (half + 1)],
-                rhs=xw[:].bitcast(FP8X4), rhs_scale=xs[:, 0, :], start=True, stop=True,
-            )
-
-        for e in range(E):
-            first_layer(e, "vector" if e in (4, 5, 7) else "scalar")
-            if e == 3:
-                turn((0, 1), "scalar", 4)
-        turn((2, 3), "scalar", 5)
+        for e in range(4):
+            first_layer(e)
+        turn((0, 1), 4)
+        for e in range(4, E):
+            first_layer(e)
+        turn((2, 3), 5)
         quantize_and_multiply((0, 1))
-        turn((4, 5), "scalar", 0)
+        turn((4, 5), 0)
         quantize_and_multiply((2, 3))
-        turn((6,), "scalar", 4)
-        turn((7,), "scalar", 5)
+        turn((6,), 4)
+        turn((7,), 5)
         quantize_and_multiply((4, 5))
         quantize_and_multiply((6,))
         quantize_and_multiply((7,))
-        y_out((0, 1, 2, 3), 0, "scalar")
-        y_out((4, 5, 6), 0, "scalar")
-        y_out((7,), 0, "vector")
+        y_out(0, 0, nc.scalar.copy)
+        y_out(0, 1, nc.scalar.copy)
+        y_out(0, 2, nc.vector.tensor_copy)
         second_layer(range(E), 1)
-        base_t = bank(4, [P, 4, P], "base_t")
-        for j in range(4):
+
+        base_low_sums = bank(4, [P, T // P, P], "base_low_sums")
+        for j in range(T // P):
             nc.tensor.matmul_mx(
-                out=base_t[:, j, :], lhsT=xw[:, j * P : (j + 1) * P].bitcast(FP8X4), lhsT_scale=xs[:, 0, j * P : (j + 1) * P],
-                rhs=ww[:, 0:P].bitcast(FP8X4), rhs_scale=ws[:, 0, 0:P], start=True, stop=True,
+                out=base_low_sums[:, j, :],
+                lhsT=x_w[:, j * P : (j + 1) * P].bitcast(FP8X4),
+                lhsT_scale=x_plane[:, j * P : (j + 1) * P],
+                rhs=w_w[:, 0:P].bitcast(FP8X4),
+                rhs_scale=w_plane[:, 0:P],
+                start=True,
+                stop=True,
             )
-        frozen_layer(1, 5)
-        y_out((0, 1, 2, 3), 1, "scalar")
-        y_out((4, 5, 6, 7), 1, "scalar")
+        base_high = bank(5, [P, T], "base_high")
+        nc.tensor.matmul_mx(
+            out=base_high[:],
+            lhsT=w_w[:, P:N].bitcast(FP8X4),
+            lhsT_scale=w_plane[:, P:N],
+            rhs=x_w[:].bitcast(FP8X4),
+            rhs_scale=x_plane[:],
+            start=True,
+            stop=True,
+        )
+        y_out(1, 0, nc.scalar.copy)
+        y_out(1, 1, nc.scalar.copy)
 
-        a = [keep.tile([P, T], F32, name="a%d" % half) for half in range(2)]
-        b = [keep.tile([P, T], F32, name="b%d" % half) for half in range(2)]
-        s = [keep.tile([P, T], F32, name="s%d" % half) for half in range(2)]
+        gated = [[keep.tile([P, T], F32, name="gated%d_%d" % (r, half)) for half in range(2)] for r in range(2)]
+        partial_high = keep.tile([P, T], F32, name="partial_high")
+        base_low = keep.tile([P, T // P, P], F32, name="base_low")
+        nc.scalar.copy(base_low[:], base_low_sums[:])
 
-        def fetch(dst, half, r, t0, t1):
-            lst = (pos1_t, pos2_t)[r]
-            nc.vector.tensor_tensor(
-                dst[half][:, t0:t1], ys[half][:].indirect(lst[:, t0 // PER_COL : t1 // PER_COL]), gate_t[:, r, t0:t1], MULT
-            )
+        def fetch(r, half, t0, t1):
+            entries = pos_t[r][:, t0 // LIST_COLUMN : t1 // LIST_COLUMN]
+            nc.vector.tensor_tensor(gated[r][half][:, t0:t1], y[half][:].indirect(entries), gate_t[:, r, t0:t1], MULT)
 
-        def finish(half, t0, t1):
-            o = keep.tile([P, t1 - t0], F32, name="o%d_%d" % (half, t0))
-            nc.vector.tensor_tensor(o[:], s[half][:, t0:t1], b[half][:, t0:t1], ADD)
-            nc.sync.dma_start(out=out[P * half : P * (half + 1), t0:t1], in_=o[:])
+        def add_transposed(sums, terms):
+            for i, term in enumerate(terms):
+                nc.tensor.matmul(
+                    sums, lhsT=term, rhs=ident[:], is_transpose=True, start=(i == 0), stop=(i == len(terms) - 1)
+                )
 
-        base_sb = keep.tile([P, 4, P], F32, name="base_sb")
-        nc.scalar.copy(base_sb[:], base_t[:])
-
-        def add_on_tensor(t0, b1, b2):
-            p1 = bank(b1, [P, 2, P], "sum_t%d" % t0)
+        def finish_low(t0, first_bank, second_bank):
+            routed_sums = bank(first_bank, [P, 2, P], "routed_sums%d" % t0)
             for j in range(2):
-                cols = slice(t0 + j * P, t0 + (j + 1) * P)
-                for i, src in enumerate((a[0], b[0])):
-                    nc.tensor.matmul(p1[:, j, :], lhsT=src[:, cols], rhs=ident[:], is_transpose=True, start=(i == 0), stop=(i == 1))
-            m = keep.tile([P, 2, P], F32, name="m%d" % t0)
-            nc.scalar.copy(m[:], p1[:])
-            p2 = bank(b2, [P, 2, P], "sum%d" % t0)
+                tokens = slice(t0 + j * P, t0 + (j + 1) * P)
+                add_transposed(routed_sums[:, j, :], (gated[0][0][:, tokens], gated[1][0][:, tokens]))
+            routed = keep.tile([P, 2, P], F32, name="routed%d" % t0)
+            nc.scalar.copy(routed[:], routed_sums[:])
+            total = bank(second_bank, [P, 2, P], "total%d" % t0)
             for j in range(2):
-                for i, src in enumerate((base_sb[:, t0 // P + j, :], m[:, j, :])):
-                    nc.tensor.matmul(p2[:, j, :], lhsT=src, rhs=ident[:], is_transpose=True, start=(i == 0), stop=(i == 1))
-            o = keep.tile([P, 2 * P], F32, name="o0_%d" % t0)
-            nc.scalar.copy(o[:], p2[:].rearrange("p j t -> p (j t)"))
-            nc.sync.dma_start(out=out[0:P, t0 : t0 + 2 * P], in_=o[:])
+                add_transposed(total[:, j, :], (base_low[:, t0 // P + j, :], routed[:, j, :]))
+            result = keep.tile([P, 2 * P], F32, name="result_low%d" % t0)
+            nc.scalar.copy(result[:], total[:].rearrange("p j t -> p (j t)"))
+            nc.sync.dma_start(out=out[0:P, t0 : t0 + 2 * P], in_=result[:])
 
-        for t0 in (0, T // 2):
-            fetch(a, 0, 0, t0, t0 + T // 2)
-            fetch(b, 0, 1, t0, t0 + T // 2)
-        fetch(a, 1, 0, 0, T)
-        fetch(b, 1, 1, 0, T // 2)
-        nc.vector.tensor_tensor(s[1][:], base[1][:], a[1][:], ADD)
-        fetch(b, 1, 1, T // 2, T)
-        add_on_tensor(0, 6, 2)
-        add_on_tensor(T // 2, 7, 0)
-        finish(1, 0, T // 2)
-        finish(1, T // 2, T)
+        def finish_high(t0, t1):
+            result = keep.tile([P, t1 - t0], F32, name="result_high%d" % t0)
+            nc.vector.tensor_tensor(result[:], partial_high[:, t0:t1], gated[1][1][:, t0:t1], ADD)
+            nc.sync.dma_start(out=out[P:N, t0:t1], in_=result[:])
+
+        middle = T // 2
+        for t0 in (0, middle):
+            fetch(0, 0, t0, t0 + middle)
+            fetch(1, 0, t0, t0 + middle)
+        fetch(0, 1, 0, T)
+        fetch(1, 1, 0, middle)
+        nc.vector.tensor_tensor(partial_high[:], base_high[:], gated[0][1][:], ADD)
+        fetch(1, 1, middle, T)
+        finish_low(0, 6, 2)
+        finish_low(middle, 7, 0)
+        finish_high(0, middle)
+        finish_high(middle, T)

@@ -22,6 +22,7 @@ RELU = mybir.ActivationFunctionType.Relu
 P = 128
 LIST_COLUMN = 16
 PAIRS = [(0, 1), (2, 3), (4, 5), (6, 7)]
+GATHER_GROUPS = [(0, 1), (2, 3, 4), (5, 6, 7)]
 PLANE_ADAPTERS = 4
 VECTOR_ZERO_WORDS = 320
 VECTOR_RELU = (4, 5, 7)
@@ -71,12 +72,12 @@ def tile_moe_adp_relu_kernel(
         ident = keep.tile([P, P], F32, name="ident")
         wa_w = [keep.tile([P, 2, 2 * H], U8, name="wa_w%d" % pair[0], align_bytes=64) for pair in PAIRS]
 
-        def load_wa_words(pair):
+        def load_wa_words(pair, queue=nc.sync):
             rows = wa_words[2 * pair : 2 * pair + 2, 0].rearrange("e p c -> p e c")
-            nc.sync.dma_start(out=wa_w[pair][:].bitcast(I32), in_=rows.bitcast(I32))
+            queue.dma_start(out=wa_w[pair][:].bitcast(I32), in_=rows.bitcast(I32))
 
         def load_wa_plane(g):
-            load_scale_rows(both_queues, wa_planes[g], wa_scales[PLANE_ADAPTERS * g : PLANE_ADAPTERS * (g + 1), 0])
+            load_scale_rows(sync_queue, wa_planes[g], wa_scales[PLANE_ADAPTERS * g : PLANE_ADAPTERS * (g + 1), 0])
 
         for plane in wa_planes:
             words = plane[:].rearrange("p e c -> p (e c)").bitcast(I32)
@@ -87,10 +88,10 @@ def tile_moe_adp_relu_kernel(
 
         both_queues = (nc.sync, nc.scalar, nc.sync, nc.scalar)
         sync_queue = (nc.sync,) * 4
+        nc.sync.dma_start(offs_t[:], offs)
         fill_scale_plane(both_queues, x_plane, x_scales[0])
         nc.scalar.dma_start(out=x_w[:].bitcast(I32), in_=x_words[0].rearrange("p t d -> p (t d)").bitcast(I32))
-        nc.sync.dma_start(offs_t[:], offs)
-        load_wa_words(0)
+        load_wa_words(0, nc.scalar)
         load_wa_plane(0)
         load_wa_words(1)
         load_wa_words(2)
@@ -105,13 +106,13 @@ def tile_moe_adp_relu_kernel(
         nc.sync.dma_start(out=gate_t[:], in_=gate.rearrange("r p t -> p r t"))
 
         slot_w, slot_plane = {}, {}
-        for pair in PAIRS:
-            words = keep.tile([P, 2 * C], U32, name="slot_w%d" % pair[0], align_bytes=64)
-            plane = keep.tile([P, 2 * C], U8, name="slot_plane%d" % pair[0], align_bytes=64)
-            entries = offs_t[:, pair[0] * C // LIST_COLUMN : (pair[0] + 2) * C // LIST_COLUMN]
-            nc.vector.tensor_copy(words[:], x_w[:].indirect(entries))
+        for group in GATHER_GROUPS:
+            words = keep.tile([P, len(group) * C], U32, name="slot_w%d" % group[0], align_bytes=64)
+            plane = keep.tile([P, len(group) * C], U8, name="slot_plane%d" % group[0], align_bytes=64)
+            entries = offs_t[:, group[0] * C // LIST_COLUMN : (group[-1] + 1) * C // LIST_COLUMN]
             nc.vector.tensor_copy(plane[:], x_plane[:].indirect(entries))
-            for x, e in enumerate(pair):
+            nc.vector.tensor_copy(words[:], x_w[:].indirect(entries))
+            for x, e in enumerate(group):
                 slot_w[e] = words[:, x * C : (x + 1) * C]
                 slot_plane[e] = plane[:, x * C : (x + 1) * C]
 
@@ -242,7 +243,7 @@ def tile_moe_adp_relu_kernel(
                     sums, lhsT=term, rhs=ident[:], is_transpose=True, start=(i == 0), stop=(i == len(terms) - 1)
                 )
 
-        def finish_low(t0, first_bank, second_bank):
+        def finish_low(t0, first_bank, second_bank, queue):
             routed_sums = bank(first_bank, [P, 2, P], "routed_sums%d" % t0)
             for j in range(2):
                 tokens = slice(t0 + j * P, t0 + (j + 1) * P)
@@ -254,7 +255,7 @@ def tile_moe_adp_relu_kernel(
                 add_transposed(total[:, j, :], (base_low[:, t0 // P + j, :], routed[:, j, :]))
             result = keep.tile([P, 2 * P], F32, name="result_low%d" % t0)
             nc.scalar.copy(result[:], total[:].rearrange("p j t -> p (j t)"))
-            nc.sync.dma_start(out=out[0:P, t0 : t0 + 2 * P], in_=result[:])
+            queue.dma_start(out=out[0:P, t0 : t0 + 2 * P], in_=result[:])
 
         def finish_high(t0, t1):
             result = keep.tile([P, t1 - t0], F32, name="result_high%d" % t0)
@@ -269,7 +270,7 @@ def tile_moe_adp_relu_kernel(
         fetch(1, 1, 0, middle)
         nc.vector.tensor_tensor(partial_high[:], base_high[:], gated[0][1][:], ADD)
         fetch(1, 1, middle, T)
-        finish_low(0, 6, 2)
-        finish_low(middle, 7, 0)
+        finish_low(0, 6, 2, nc.scalar)
+        finish_low(middle, 7, 0, nc.scalar)
         finish_high(0, middle)
         finish_high(middle, T)

@@ -22,11 +22,11 @@ RELU = mybir.ActivationFunctionType.Relu
 P = 128
 LIST_COLUMN = 16
 PAIRS = [(0, 1), (2, 3), (4, 5), (6, 7)]
-GATHER_GROUPS = [(0, 1), (2, 3, 4), (5, 6, 7)]
+GATHER_GROUPS = [(0, 2), (2, 5), (5, E)]
+LAST_STORE = 320
 PLANE_ADAPTERS = 4
-VECTOR_ZERO_WORDS = 320
 VECTOR_RELU = (4, 5, 7)
-Y_GROUPS = [[((0, 1, 2, 3), 6), ((4, 5, 6), 7), ((7,), 2)], [((0, 1, 2, 3), 1), ((4, 5, 6, 7), 3)]]
+Y_GROUPS = [[((0, 1, 2, 3), 6), ((4, 5), 7), ((6,), 0), ((7,), 2)], [((0, 1, 2, 3), 1), ((4, 5, 6, 7), 3)]]
 
 
 def load_scale_rows(queues, plane, rows):
@@ -80,9 +80,7 @@ def tile_moe_adp_relu_kernel(
             load_scale_rows(sync_queue, wa_planes[g], wa_scales[PLANE_ADAPTERS * g : PLANE_ADAPTERS * (g + 1), 0])
 
         for plane in wa_planes:
-            words = plane[:].rearrange("p e c -> p (e c)").bitcast(I32)
-            nc.vector.memset(words[:, 0:VECTOR_ZERO_WORDS], 0)
-            nc.gpsimd.memset(words[:, VECTOR_ZERO_WORDS:], 0)
+            nc.vector.memset(plane[:].bitcast(I32), 0)
         nc.vector.memset(wb_plane[:].bitcast(I32), 0)
         make_identity(nc, ident[:])
 
@@ -106,15 +104,18 @@ def tile_moe_adp_relu_kernel(
         nc.sync.dma_start(out=gate_t[:], in_=gate.rearrange("r p t -> p r t"))
 
         slot_w, slot_plane = {}, {}
-        for group in GATHER_GROUPS:
-            words = keep.tile([P, len(group) * C], U32, name="slot_w%d" % group[0], align_bytes=64)
-            plane = keep.tile([P, len(group) * C], U8, name="slot_plane%d" % group[0], align_bytes=64)
-            entries = offs_t[:, group[0] * C // LIST_COLUMN : (group[-1] + 1) * C // LIST_COLUMN]
-            nc.vector.tensor_copy(plane[:], x_plane[:].indirect(entries))
-            nc.vector.tensor_copy(words[:], x_w[:].indirect(entries))
-            for x, e in enumerate(group):
-                slot_w[e] = words[:, x * C : (x + 1) * C]
-                slot_plane[e] = plane[:, x * C : (x + 1) * C]
+
+        def gather(source, dtype, slots, name, e0, e1):
+            picked = keep.tile([P, (e1 - e0) * C], dtype, name="%s%d" % (name, e0), align_bytes=64)
+            entries = offs_t[:, e0 * C // LIST_COLUMN : e1 * C // LIST_COLUMN]
+            nc.vector.tensor_copy(picked[:], source[:].indirect(entries))
+            for e in range(e0, e1):
+                slots[e] = picked[:, (e - e0) * C : (e - e0 + 1) * C]
+
+        for e0, e1 in GATHER_GROUPS:
+            gather(x_plane, U8, slot_plane, "slot_plane", e0, e1)
+            gather(x_w, U32, slot_w, "slot_w", e0, min(e1, E - 1))
+        gather(x_w, U32, slot_w, "slot_w", E - 1, E)
 
         h_rows = {}
 
@@ -200,8 +201,9 @@ def tile_moe_adp_relu_kernel(
         quantize_and_multiply((6,))
         quantize_and_multiply((7,))
         y_out(0, 0, nc.scalar.copy)
-        y_out(0, 1, nc.scalar.copy)
-        y_out(0, 2, nc.vector.tensor_copy)
+        y_out(0, 1, nc.vector.tensor_copy)
+        y_out(0, 2, nc.scalar.copy)
+        y_out(0, 3, nc.scalar.copy)
         second_layer(range(E), 1)
 
         base_low_sums = bank(4, [P, T // P, P], "base_low_sums")
@@ -263,14 +265,14 @@ def tile_moe_adp_relu_kernel(
             nc.sync.dma_start(out=out[P:N, t0:t1], in_=result[:])
 
         middle = T // 2
+        fetch(0, 0, 0, T)
         for t0 in (0, middle):
-            fetch(0, 0, t0, t0 + middle)
             fetch(1, 0, t0, t0 + middle)
         fetch(0, 1, 0, T)
-        fetch(1, 1, 0, middle)
+        fetch(1, 1, 0, LAST_STORE)
         nc.vector.tensor_tensor(partial_high[:], base_high[:], gated[0][1][:], ADD)
-        fetch(1, 1, middle, T)
+        fetch(1, 1, LAST_STORE, T)
         finish_low(0, 6, 2, nc.scalar)
         finish_low(middle, 7, 0, nc.scalar)
-        finish_high(0, middle)
-        finish_high(middle, T)
+        finish_high(0, LAST_STORE)
+        finish_high(LAST_STORE, T)

@@ -21,12 +21,11 @@ RELU = mybir.ActivationFunctionType.Relu
 
 P = 128
 LIST_COLUMN = 16
-PAIRS = [(0, 1), (2, 3), (4, 5), (6, 7)]
 GATHER_GROUPS = [(0, 2), (2, 5), (5, E)]
 LAST_STORE = 320
 PLANE_ADAPTERS = 4
 VECTOR_RELU = (4, 5, 7)
-Y_GROUPS = [[((0, 1, 2, 3), 6), ((4, 5), 7), ((6,), 0), ((7,), 2)], [((0, 1, 2, 3), 1), ((4, 5, 6, 7), 3)]]
+Y_GROUPS = [[((0, 1, 2, 3), 6), ((4, 5), 7), ((6,), 2), ((7,), 3)], [((0, 1, 2, 3), 5), ((4, 5, 6, 7), 4)]]
 
 
 def load_scale_rows(queues, plane, rows):
@@ -70,11 +69,13 @@ def tile_moe_adp_relu_kernel(
         wb_w = keep.tile([P, E, 2 * N], U8, name="wb_w", align_bytes=64)
         gate_t = keep.tile([P, 2, T], F32, name="gate_t")
         ident = keep.tile([P, P], F32, name="ident")
-        wa_w = [keep.tile([P, 2, 2 * H], U8, name="wa_w%d" % pair[0], align_bytes=64) for pair in PAIRS]
+        wa_w = [
+            keep.tile([P, PLANE_ADAPTERS, 2 * H], U8, name="wa_w%d" % g, align_bytes=64) for g in range(E // PLANE_ADAPTERS)
+        ]
 
-        def load_wa_words(pair, queue=nc.sync):
-            rows = wa_words[2 * pair : 2 * pair + 2, 0].rearrange("e p c -> p e c")
-            queue.dma_start(out=wa_w[pair][:].bitcast(I32), in_=rows.bitcast(I32))
+        def load_wa_words(g, queue):
+            rows = wa_words[PLANE_ADAPTERS * g : PLANE_ADAPTERS * (g + 1), 0].rearrange("e p c -> p e c")
+            queue.dma_start(out=wa_w[g][:].bitcast(I32), in_=rows.bitcast(I32))
 
         def load_wa_plane(g):
             load_scale_rows(sync_queue, wa_planes[g], wa_scales[PLANE_ADAPTERS * g : PLANE_ADAPTERS * (g + 1), 0])
@@ -91,10 +92,8 @@ def tile_moe_adp_relu_kernel(
         nc.scalar.dma_start(out=x_w[:].bitcast(I32), in_=x_words[0].rearrange("p t d -> p (t d)").bitcast(I32))
         load_wa_words(0, nc.scalar)
         load_wa_plane(0)
-        load_wa_words(1)
-        load_wa_words(2)
+        load_wa_words(1, nc.sync)
         load_wa_plane(1)
-        load_wa_words(3)
         nc.sync.dma_start(out=wb_w[:].bitcast(I32), in_=wb_words[:, 0].rearrange("e p c -> p e c").bitcast(I32))
         load_scale_rows(sync_queue, wb_plane, wb_scales[:, 0])
         nc.sync.dma_start(out=w_w[:].bitcast(I32), in_=w_words[0].rearrange("p n d -> p (n d)").bitcast(I32))
@@ -120,12 +119,12 @@ def tile_moe_adp_relu_kernel(
         h_rows = {}
 
         def first_layer(e):
-            sums = bank(e % 4, [P, H], "h_sums%d" % e)
+            sums = bank(e % 6, [P, H], "h_sums%d" % e)
             nc.tensor.matmul_mx(
                 out=sums[:],
                 lhsT=slot_w[e].bitcast(FP8X4),
                 lhsT_scale=slot_plane[e],
-                rhs=wa_w[e // 2][:, e % 2, :].bitcast(FP4X4),
+                rhs=wa_w[e // PLANE_ADAPTERS][:, e % PLANE_ADAPTERS, :].bitcast(FP4X4),
                 rhs_scale=wa_planes[e // PLANE_ADAPTERS][:, e % PLANE_ADAPTERS, :],
                 start=True,
                 stop=True,
@@ -186,17 +185,17 @@ def tile_moe_adp_relu_kernel(
             members = Y_GROUPS[half][index][0]
             copy(y[half][:, members[0] * C : (members[-1] + 1) * C], y_sums[(members, half)][:])
 
-        for e in range(4):
+        for e in range(6):
             first_layer(e)
-        turn((0, 1), 4)
-        for e in range(4, E):
+        turn((0, 1), 2)
+        for e in range(6, E):
             first_layer(e)
-        turn((2, 3), 5)
+        turn((2, 3), 3)
         quantize_and_multiply((0, 1))
-        turn((4, 5), 0)
+        turn((4, 5), 4)
         quantize_and_multiply((2, 3))
-        turn((6,), 4)
-        turn((7,), 5)
+        turn((6,), 0)
+        turn((7,), 1)
         quantize_and_multiply((4, 5))
         quantize_and_multiply((6,))
         quantize_and_multiply((7,))
@@ -206,7 +205,7 @@ def tile_moe_adp_relu_kernel(
         y_out(0, 3, nc.scalar.copy)
         second_layer(range(E), 1)
 
-        base_low_sums = bank(4, [P, T // P, P], "base_low_sums")
+        base_low_sums = bank(0, [P, T // P, P], "base_low_sums")
         for j in range(T // P):
             nc.tensor.matmul_mx(
                 out=base_low_sums[:, j, :],
@@ -217,7 +216,7 @@ def tile_moe_adp_relu_kernel(
                 start=True,
                 stop=True,
             )
-        base_high = bank(5, [P, T], "base_high")
+        base_high = bank(1, [P, T], "base_high")
         nc.tensor.matmul_mx(
             out=base_high[:],
             lhsT=w_w[:, P:N].bitcast(FP8X4),

@@ -22,10 +22,12 @@ RELU = mybir.ActivationFunctionType.Relu
 P = 128
 LIST_COLUMN = 16
 GATHER_GROUPS = [(0, 2), (2, 5), (5, E)]
+DIRECT = (6, E)
+DIRECT_GROUP = tuple(range(DIRECT[0], DIRECT[1]))
 LAST_STORE = 320
 PLANE_ADAPTERS = 4
-VECTOR_RELU = (4, 5, 7)
-Y_GROUPS = [[((0, 1, 2, 3), 6), ((4, 5), 7), ((6,), 2), ((7,), 3)], [((0, 1, 2, 3), 5), ((4, 5, 6, 7), 4)]]
+VECTOR_RELU = (4, 7)
+Y_GROUPS = [[((0, 1, 2, 3), 1), ((6, 7), 4), ((4, 5), 5)], [((0, 1, 2, 3), 2), ((4, 5, 6, 7), 3)]]
 
 
 def load_scale_rows(queues, plane, rows):
@@ -104,8 +106,9 @@ def tile_moe_adp_relu_kernel(
 
         slot_w, slot_plane = {}, {}
 
-        def gather(source, dtype, slots, name, e0, e1):
-            picked = keep.tile([P, (e1 - e0) * C], dtype, name="%s%d" % (name, e0), align_bytes=64)
+        def gather(source, dtype, slots, name, e0, e1, tag=None):
+            name = "%s%d" % (name, e0)
+            picked = keep.tile([P, (e1 - e0) * C], dtype, name=name, tag=tag or name, align_bytes=64)
             entries = offs_t[:, e0 * C // LIST_COLUMN : e1 * C // LIST_COLUMN]
             nc.vector.tensor_copy(picked[:], source[:].indirect(entries))
             for e in range(e0, e1):
@@ -116,10 +119,25 @@ def tile_moe_adp_relu_kernel(
             gather(x_w, U32, slot_w, "slot_w", e0, min(e1, E - 1))
         gather(x_w, U32, slot_w, "slot_w", E - 1, E)
 
+        direct = DIRECT[1] - DIRECT[0]
+        sorted_w = keep.tile([P, direct, H], U16, name="sorted_w", align_bytes=64)
+        first = DIRECT[0] - PLANE_ADAPTERS
+        nc.gpsimd.tensor_copy(
+            sorted_w[:].rearrange("p e (d m) -> p e d m", d=4),
+            wa_w[1][:, first : first + direct, :].bitcast(U16).rearrange("p e (m d) -> p e d m", d=4),
+        )
+        sorted_plane = {}
+        for e in DIRECT_GROUP:
+            sorted_plane[e] = keep.tile([P, H], U8, name="sorted_plane%d" % e, align_bytes=64)
+            nc.gpsimd.tensor_copy(
+                sorted_plane[e][:].rearrange("p (d m) -> p d m", d=4),
+                wa_planes[1][:, e - PLANE_ADAPTERS, :].rearrange("p (m d) -> p d m", d=4),
+            )
+
         h_rows = {}
 
-        def first_layer(e):
-            sums = bank(e % 6, [P, H], "h_sums%d" % e)
+        def first_layer(e, number):
+            sums = bank(number, [P, H], "h_sums%d" % e)
             nc.tensor.matmul_mx(
                 out=sums[:],
                 lhsT=slot_w[e].bitcast(FP8X4),
@@ -137,9 +155,28 @@ def tile_moe_adp_relu_kernel(
             else:
                 nc.scalar.activation(dst, src, RELU)
 
-        h_turned = {}
+        h_turned = {DIRECT_GROUP: keep.tile([P, direct * C * 4], BF16, name="h_direct", align_bytes=64)}
 
-        def turn(group, number):
+        def direct_layer(e, number):
+            sums = bank(number, [P, 4, C], "h_sums%d" % e)
+            for d in range(4):
+                nc.tensor.matmul_mx(
+                    out=sums[:, d, :],
+                    lhsT=sorted_w[:, e - DIRECT[0], d * P : (d + 1) * P].bitcast(FP4X4),
+                    lhsT_scale=sorted_plane[e][:, d * P : (d + 1) * P],
+                    rhs=slot_w[e].bitcast(FP8X4),
+                    rhs_scale=slot_plane[e],
+                    start=True,
+                    stop=True,
+                )
+            dst = h_turned[DIRECT_GROUP][:, (e - DIRECT[0]) * H : (e - DIRECT[0] + 1) * H].rearrange("p (s d) -> p s d", d=4)
+            src = sums[:].rearrange("p d s -> p s d")
+            if e in VECTOR_RELU:
+                nc.vector.tensor_scalar_max(dst, src, 0.0)
+            else:
+                nc.scalar.activation(dst, src, RELU)
+
+        def turn(group, number, copy):
             count = len(group)
             pairs = bank(number, [P, 2, 2, C], "h_pairs%d" % group[0])
             for x, e in enumerate(group):
@@ -147,7 +184,7 @@ def tile_moe_adp_relu_kernel(
                 for u in range(2):
                     nc.tensor.transpose(pairs[:, x, u, :], words[:, u * P : (u + 1) * P], ident[:])
             h_turned[group] = keep.tile([P, count * C * 4], BF16, name="h_turned%d" % group[0], align_bytes=64)
-            nc.scalar.copy(
+            copy(
                 h_turned[group][:].bitcast(F32).rearrange("p (x s u) -> p x s u", x=count, u=2),
                 pairs[:, 0:count, :, :].rearrange("p x u s -> p x s u"),
             )
@@ -185,27 +222,23 @@ def tile_moe_adp_relu_kernel(
             members = Y_GROUPS[half][index][0]
             copy(y[half][:, members[0] * C : (members[-1] + 1) * C], y_sums[(members, half)][:])
 
-        for e in range(6):
-            first_layer(e)
-        turn((0, 1), 2)
-        for e in range(6, E):
-            first_layer(e)
-        turn((2, 3), 3)
+        for e in range(DIRECT[0]):
+            first_layer(e, e)
+        turn((0, 1), 2, nc.vector.tensor_copy)
+        turn((2, 3), 3, nc.scalar.copy)
         quantize_and_multiply((0, 1))
-        turn((4, 5), 4)
+        direct_layer(6, 6)
+        direct_layer(7, 7)
+        turn((4, 5), 0, nc.scalar.copy)
         quantize_and_multiply((2, 3))
-        turn((6,), 0)
-        turn((7,), 1)
+        quantize_and_multiply((6, 7))
         quantize_and_multiply((4, 5))
-        quantize_and_multiply((6,))
-        quantize_and_multiply((7,))
         y_out(0, 0, nc.scalar.copy)
         y_out(0, 1, nc.vector.tensor_copy)
         y_out(0, 2, nc.scalar.copy)
-        y_out(0, 3, nc.scalar.copy)
         second_layer(range(E), 1)
 
-        base_low_sums = bank(0, [P, T // P, P], "base_low_sums")
+        base_low_sums = bank(6, [P, T // P, P], "base_low_sums")
         for j in range(T // P):
             nc.tensor.matmul_mx(
                 out=base_low_sums[:, j, :],
@@ -216,7 +249,7 @@ def tile_moe_adp_relu_kernel(
                 start=True,
                 stop=True,
             )
-        base_high = bank(1, [P, T], "base_high")
+        base_high = bank(7, [P, T], "base_high")
         nc.tensor.matmul_mx(
             out=base_high[:],
             lhsT=w_w[:, P:N].bitcast(FP8X4),
@@ -271,7 +304,7 @@ def tile_moe_adp_relu_kernel(
         fetch(1, 1, 0, LAST_STORE)
         nc.vector.tensor_tensor(partial_high[:], base_high[:], gated[0][1][:], ADD)
         fetch(1, 1, LAST_STORE, T)
-        finish_low(0, 6, 2, nc.scalar)
-        finish_low(middle, 7, 0, nc.scalar)
+        finish_low(0, 1, 4, nc.scalar)
+        finish_low(middle, 5, 0, nc.scalar)
         finish_high(0, LAST_STORE)
         finish_high(LAST_STORE, T)

@@ -21,13 +21,11 @@ RELU = mybir.ActivationFunctionType.Relu
 
 P = 128
 LIST_COLUMN = 16
-GATHER_GROUPS = [(0, 2), (2, 5), (5, E)]
-DIRECT = (6, E)
-DIRECT_GROUP = tuple(range(DIRECT[0], DIRECT[1]))
+DIRECT_GROUP = (0, E - 1)
 LAST_STORE = 320
 PLANE_ADAPTERS = 4
-VECTOR_RELU = (4, 7)
-Y_GROUPS = [[((0, 1, 2, 3), 1), ((6, 7), 4), ((4, 5), 5)], [((0, 1, 2, 3), 2), ((4, 5, 6, 7), 3)]]
+VECTOR_RELU = (5, 0)
+Y_GROUPS = [[((1, 2, 3, 4), 1), ((0, 7), 4), ((5, 6), 5)], [((0, 1, 2, 3), 2), ((4, 5, 6, 7), 3)]]
 
 
 def load_scale_rows(queues, plane, rows):
@@ -114,25 +112,21 @@ def tile_moe_adp_relu_kernel(
             for e in range(e0, e1):
                 slots[e] = picked[:, (e - e0) * C : (e - e0 + 1) * C]
 
-        for e0, e1 in GATHER_GROUPS:
+        gather(x_plane, U8, slot_plane, "slot_plane", 0, 3)
+        gather(x_w, U32, slot_w, "slot_w", 1, 3)
+        for e0, e1 in ((3, 6), (6, E)):
             gather(x_plane, U8, slot_plane, "slot_plane", e0, e1)
-            gather(x_w, U32, slot_w, "slot_w", e0, min(e1, E - 1))
-        gather(x_w, U32, slot_w, "slot_w", E - 1, E)
+            gather(x_w, U32, slot_w, "slot_w", e0, e1)
+        gather(x_w, U32, slot_w, "slot_w", 0, 1)
 
-        direct = DIRECT[1] - DIRECT[0]
-        sorted_w = keep.tile([P, direct, H], U16, name="sorted_w", align_bytes=64)
-        first = DIRECT[0] - PLANE_ADAPTERS
-        nc.gpsimd.tensor_copy(
-            sorted_w[:].rearrange("p e (d m) -> p e d m", d=4),
-            wa_w[1][:, first : first + direct, :].bitcast(U16).rearrange("p e (m d) -> p e d m", d=4),
-        )
-        sorted_plane = {}
+        direct = len(DIRECT_GROUP)
+        sorted_w, sorted_plane = {}, {}
         for e in DIRECT_GROUP:
+            g, x = divmod(e, PLANE_ADAPTERS)
+            sorted_w[e] = keep.tile([P, H], U16, name="sorted_w%d" % e, align_bytes=64)
             sorted_plane[e] = keep.tile([P, H], U8, name="sorted_plane%d" % e, align_bytes=64)
-            nc.gpsimd.tensor_copy(
-                sorted_plane[e][:].rearrange("p (d m) -> p d m", d=4),
-                wa_planes[1][:, e - PLANE_ADAPTERS, :].rearrange("p (m d) -> p d m", d=4),
-            )
+            for dst, src in ((sorted_w[e], wa_w[g][:, x, :].bitcast(U16)), (sorted_plane[e], wa_planes[g][:, x, :])):
+                nc.gpsimd.tensor_copy(dst[:].rearrange("p (d m) -> p d m", d=4), src.rearrange("p (m d) -> p d m", d=4))
 
         h_rows = {}
 
@@ -162,14 +156,14 @@ def tile_moe_adp_relu_kernel(
             for d in range(4):
                 nc.tensor.matmul_mx(
                     out=sums[:, d, :],
-                    lhsT=sorted_w[:, e - DIRECT[0], d * P : (d + 1) * P].bitcast(FP4X4),
+                    lhsT=sorted_w[e][:, d * P : (d + 1) * P].bitcast(FP4X4),
                     lhsT_scale=sorted_plane[e][:, d * P : (d + 1) * P],
                     rhs=slot_w[e].bitcast(FP8X4),
                     rhs_scale=slot_plane[e],
                     start=True,
                     stop=True,
                 )
-            dst = h_turned[DIRECT_GROUP][:, (e - DIRECT[0]) * H : (e - DIRECT[0] + 1) * H].rearrange("p (s d) -> p s d", d=4)
+            dst = h_turned[DIRECT_GROUP][:, DIRECT_GROUP.index(e) * H : (DIRECT_GROUP.index(e) + 1) * H].rearrange("p (s d) -> p s d", d=4)
             src = sums[:].rearrange("p d s -> p s d")
             if e in VECTOR_RELU:
                 nc.vector.tensor_scalar_max(dst, src, 0.0)
@@ -196,7 +190,7 @@ def tile_moe_adp_relu_kernel(
                 members, number = [g for g in Y_GROUPS[half] if e in g[0]][0]
                 if (members, half) not in y_sums:
                     y_sums[(members, half)] = bank(number, [P, len(members) * C], "y_sums%d_%d" % (half, members[0]))
-                x = e - members[0]
+                x = members.index(e)
                 nc.tensor.matmul_mx(
                     out=y_sums[(members, half)][:, x * C : (x + 1) * C],
                     lhsT=wb_w[:, e, 2 * P * half : 2 * P * (half + 1)].bitcast(FP4X4),
@@ -220,19 +214,23 @@ def tile_moe_adp_relu_kernel(
 
         def y_out(half, index, copy):
             members = Y_GROUPS[half][index][0]
-            copy(y[half][:, members[0] * C : (members[-1] + 1) * C], y_sums[(members, half)][:])
+            chosen = slice(members[0], members[-1] + 1, members[1] - members[0])
+            copy(
+                y[half][:].rearrange("p (e c) -> p e c", c=C)[:, chosen, :],
+                y_sums[(members, half)][:].rearrange("p (e c) -> p e c", c=C),
+            )
 
-        for e in range(DIRECT[0]):
-            first_layer(e, e)
-        turn((0, 1), 2, nc.vector.tensor_copy)
-        turn((2, 3), 3, nc.scalar.copy)
-        quantize_and_multiply((0, 1))
-        direct_layer(6, 6)
-        direct_layer(7, 7)
-        turn((4, 5), 0, nc.scalar.copy)
-        quantize_and_multiply((2, 3))
-        quantize_and_multiply((6, 7))
-        quantize_and_multiply((4, 5))
+        for e in range(1, E - 1):
+            first_layer(e, e - 1)
+        turn((1, 2), 2, nc.vector.tensor_copy)
+        turn((3, 4), 0, nc.scalar.copy)
+        quantize_and_multiply((1, 2))
+        direct_layer(7, 6)
+        direct_layer(0, 3)
+        turn((5, 6), 7, nc.scalar.copy)
+        quantize_and_multiply((3, 4))
+        quantize_and_multiply(DIRECT_GROUP)
+        quantize_and_multiply((5, 6))
         y_out(0, 0, nc.scalar.copy)
         y_out(0, 1, nc.vector.tensor_copy)
         y_out(0, 2, nc.scalar.copy)
@@ -249,7 +247,7 @@ def tile_moe_adp_relu_kernel(
                 start=True,
                 stop=True,
             )
-        base_high = bank(7, [P, T], "base_high")
+        base_high = bank(0, [P, T], "base_high")
         nc.tensor.matmul_mx(
             out=base_high[:],
             lhsT=w_w[:, P:N].bitcast(FP8X4),
@@ -305,6 +303,6 @@ def tile_moe_adp_relu_kernel(
         nc.vector.tensor_tensor(partial_high[:], base_high[:], gated[0][1][:], ADD)
         fetch(1, 1, LAST_STORE, T)
         finish_low(0, 1, 4, nc.scalar)
-        finish_low(middle, 5, 0, nc.scalar)
+        finish_low(middle, 5, 7, nc.scalar)
         finish_high(0, LAST_STORE)
         finish_high(LAST_STORE, T)

@@ -25,7 +25,7 @@ DIRECT_GROUP = (0, E - 1)
 LAST_STORE = 320
 PLANE_ADAPTERS = 4
 VECTOR_RELU = (5, 0)
-Y_GROUPS = [[((1, 2, 3, 4), 1), ((0, 7), 4), ((5, 6), 5)], [((0, 1, 2, 3), 2), ((4, 5, 6, 7), 3)]]
+Y_GROUPS = [[((1, 2, 3, 4), 1), ((0, 7), 4), ((5,), 5), ((6,), 6)], [((0, 1, 2, 3), 2), ((4, 5, 6, 7), 3)]]
 
 
 def load_scale_rows(queues, plane, rows):
@@ -112,12 +112,9 @@ def tile_moe_adp_relu_kernel(
             for e in range(e0, e1):
                 slots[e] = picked[:, (e - e0) * C : (e - e0 + 1) * C]
 
-        gather(x_plane, U8, slot_plane, "slot_plane", 0, 3)
-        gather(x_w, U32, slot_w, "slot_w", 1, 3)
-        for e0, e1 in ((3, 6), (6, E)):
+        for e0, e1 in ((1, 3), (3, 6), (6, E), (0, 1)):
             gather(x_plane, U8, slot_plane, "slot_plane", e0, e1)
             gather(x_w, U32, slot_w, "slot_w", e0, e1)
-        gather(x_w, U32, slot_w, "slot_w", 0, 1)
 
         direct = len(DIRECT_GROUP)
         sorted_w, sorted_plane = {}, {}
@@ -214,7 +211,7 @@ def tile_moe_adp_relu_kernel(
 
         def y_out(half, index, copy):
             members = Y_GROUPS[half][index][0]
-            chosen = slice(members[0], members[-1] + 1, members[1] - members[0])
+            chosen = slice(members[0], members[-1] + 1, members[1] - members[0] if len(members) > 1 else 1)
             copy(
                 y[half][:].rearrange("p (e c) -> p e c", c=C)[:, chosen, :],
                 y_sums[(members, half)][:].rearrange("p (e c) -> p e c", c=C),
@@ -227,16 +224,19 @@ def tile_moe_adp_relu_kernel(
         quantize_and_multiply((1, 2))
         direct_layer(7, 6)
         direct_layer(0, 3)
-        turn((5, 6), 7, nc.scalar.copy)
         quantize_and_multiply((3, 4))
+        turn((5,), 7, nc.vector.tensor_copy)
+        turn((6,), 2, nc.scalar.copy)
         quantize_and_multiply(DIRECT_GROUP)
-        quantize_and_multiply((5, 6))
+        quantize_and_multiply((5,))
+        quantize_and_multiply((6,))
         y_out(0, 0, nc.scalar.copy)
         y_out(0, 1, nc.vector.tensor_copy)
         y_out(0, 2, nc.scalar.copy)
+        y_out(0, 3, nc.scalar.copy)
         second_layer(range(E), 1)
 
-        base_low_sums = bank(6, [P, T // P, P], "base_low_sums")
+        base_low_sums = bank(7, [P, T // P, P], "base_low_sums")
         for j in range(T // P):
             nc.tensor.matmul_mx(
                 out=base_low_sums[:, j, :],
@@ -303,6 +303,6 @@ def tile_moe_adp_relu_kernel(
         nc.vector.tensor_tensor(partial_high[:], base_high[:], gated[0][1][:], ADD)
         fetch(1, 1, LAST_STORE, T)
         finish_low(0, 1, 4, nc.scalar)
-        finish_low(middle, 5, 7, nc.scalar)
+        finish_low(middle, 5, 6, nc.scalar)
         finish_high(0, LAST_STORE)
         finish_high(LAST_STORE, T)

@@ -111,10 +111,26 @@ def tile_moe_adp_relu_kernel(
             nc.vector.tensor_copy(picked[:], source[:].indirect(entries))
             for e in range(e0, e1):
                 slots[e] = picked[:, (e - e0) * C : (e - e0 + 1) * C]
+            return picked
 
+        groups = {}
         for e0, e1 in ((1, 3), (3, 6), (6, E), (0, 1)):
-            gather(x_plane, U8, slot_plane, "slot_plane", e0, e1)
-            gather(x_w, U32, slot_w, "slot_w", e0, e1)
+            groups[e0] = (
+                gather(x_plane, U8, slot_plane, "slot_plane", e0, e1),
+                gather(x_w, U32, slot_w, "slot_w", e0, e1),
+            )
+
+        warm = bank(7, [P, 2 * C], "warm")
+        for i in range(2):
+            nc.tensor.matmul_mx(
+                out=warm[:],
+                lhsT=slot_w[1].bitcast(FP8X4),
+                lhsT_scale=slot_plane[1],
+                rhs=groups[1][1][:].bitcast(FP8X4),
+                rhs_scale=groups[1][0][:],
+                start=True,
+                stop=True,
+            )
 
         direct = len(DIRECT_GROUP)
         sorted_w, sorted_plane = {}, {}

@@ -238,10 +238,10 @@ def tile_moe_adp_relu_kernel(
         turn((1, 2), 2, nc.vector.tensor_copy)
         turn((3, 4), 0, nc.scalar.copy)
         quantize_and_multiply((1, 2))
-        direct_layer(7, 6)
         direct_layer(0, 3)
+        direct_layer(7, 6)
         quantize_and_multiply((3, 4))
-        turn((5,), 7, nc.vector.tensor_copy)
+        turn((5,), 7, nc.scalar.copy)
         turn((6,), 2, nc.scalar.copy)
         quantize_and_multiply(DIRECT_GROUP)
         quantize_and_multiply((5,))

@@ -21,11 +21,13 @@ RELU = mybir.ActivationFunctionType.Relu
 
 P = 128
 LIST_COLUMN = 16
-DIRECT_GROUP = (0, E - 1)
-LAST_STORE = 320
-PLANE_ADAPTERS = 4
+BANKS = 8
+LOAD_ADAPTERS = 4
+DIRECT = (0, E - 1)
+GATHER_GROUPS = [(1, 3), (3, 6), (6, E), (0, 1)]
 VECTOR_RELU = (5, 0)
-Y_GROUPS = [[((1, 2, 3, 4), 1), ((0, 7), 4), ((5,), 5), ((6,), 6)], [((0, 1, 2, 3), 2), ((4, 5, 6, 7), 3)]]
+Y_GROUPS = [[((1, 2, 3, 4), 1), (DIRECT, 4), ((5,), 5), ((6,), 6)], [((0, 1, 2, 3), 2), ((4, 5, 6, 7), 3)]]
+LAST_STORE = 320
 
 
 def load_scale_rows(queues, plane, rows):
@@ -62,31 +64,30 @@ def tile_moe_adp_relu_kernel(
         x_plane = keep.tile([P, T], U8, name="x_plane", align_bytes=64)
         w_w = keep.tile([P, N], U32, name="w_w", align_bytes=64)
         w_plane = keep.tile([P, N], U8, name="w_plane", align_bytes=64)
-        wa_planes = [
-            keep.tile([P, PLANE_ADAPTERS, H], U8, name="wa_plane%d" % g, align_bytes=64) for g in range(E // PLANE_ADAPTERS)
-        ]
+        wa_loads = range(E // LOAD_ADAPTERS)
+        wa_planes = [keep.tile([P, LOAD_ADAPTERS, H], U8, name="wa_plane%d" % g, align_bytes=64) for g in wa_loads]
         wb_plane = keep.tile([P, E, N], U8, name="wb_plane", align_bytes=64)
         wb_w = keep.tile([P, E, 2 * N], U8, name="wb_w", align_bytes=64)
         gate_t = keep.tile([P, 2, T], F32, name="gate_t")
         ident = keep.tile([P, P], F32, name="ident")
-        wa_w = [
-            keep.tile([P, PLANE_ADAPTERS, 2 * H], U8, name="wa_w%d" % g, align_bytes=64) for g in range(E // PLANE_ADAPTERS)
-        ]
+        wa_w = [keep.tile([P, LOAD_ADAPTERS, 2 * H], U8, name="wa_w%d" % g, align_bytes=64) for g in wa_loads]
+        wa_w_of = [wa_w[e // LOAD_ADAPTERS][:, e % LOAD_ADAPTERS, :] for e in range(E)]
+        wa_plane_of = [wa_planes[e // LOAD_ADAPTERS][:, e % LOAD_ADAPTERS, :] for e in range(E)]
+        both_queues = (nc.sync, nc.scalar, nc.sync, nc.scalar)
+        sync_queue = (nc.sync,) * 4
 
         def load_wa_words(g, queue):
-            rows = wa_words[PLANE_ADAPTERS * g : PLANE_ADAPTERS * (g + 1), 0].rearrange("e p c -> p e c")
+            rows = wa_words[LOAD_ADAPTERS * g : LOAD_ADAPTERS * (g + 1), 0].rearrange("e p c -> p e c")
             queue.dma_start(out=wa_w[g][:].bitcast(I32), in_=rows.bitcast(I32))
 
         def load_wa_plane(g):
-            load_scale_rows(sync_queue, wa_planes[g], wa_scales[PLANE_ADAPTERS * g : PLANE_ADAPTERS * (g + 1), 0])
+            load_scale_rows(sync_queue, wa_planes[g], wa_scales[LOAD_ADAPTERS * g : LOAD_ADAPTERS * (g + 1), 0])
 
         for plane in wa_planes:
             nc.vector.memset(plane[:].bitcast(I32), 0)
         nc.vector.memset(wb_plane[:].bitcast(I32), 0)
         make_identity(nc, ident[:])
 
-        both_queues = (nc.sync, nc.scalar, nc.sync, nc.scalar)
-        sync_queue = (nc.sync,) * 4
         nc.sync.dma_start(offs_t[:], offs)
         fill_scale_plane(both_queues, x_plane, x_scales[0])
         nc.scalar.dma_start(out=x_w[:].bitcast(I32), in_=x_words[0].rearrange("p t d -> p (t d)").bitcast(I32))
@@ -104,65 +105,48 @@ def tile_moe_adp_relu_kernel(
 
         slot_w, slot_plane = {}, {}
 
-        def gather(source, dtype, slots, name, e0, e1, tag=None):
-            name = "%s%d" % (name, e0)
-            picked = keep.tile([P, (e1 - e0) * C], dtype, name=name, tag=tag or name, align_bytes=64)
+        def gather(source, dtype, slots, name, e0, e1):
+            picked = keep.tile([P, (e1 - e0) * C], dtype, name="%s%d" % (name, e0), align_bytes=64)
             entries = offs_t[:, e0 * C // LIST_COLUMN : e1 * C // LIST_COLUMN]
             nc.vector.tensor_copy(picked[:], source[:].indirect(entries))
             for e in range(e0, e1):
                 slots[e] = picked[:, (e - e0) * C : (e - e0 + 1) * C]
-            return picked
 
-        groups = {}
-        for e0, e1 in ((1, 3), (3, 6), (6, E), (0, 1)):
-            groups[e0] = (
-                gather(x_plane, U8, slot_plane, "slot_plane", e0, e1),
-                gather(x_w, U32, slot_w, "slot_w", e0, e1),
-            )
+        for e0, e1 in GATHER_GROUPS:
+            gather(x_plane, U8, slot_plane, "slot_plane", e0, e1)
+            gather(x_w, U32, slot_w, "slot_w", e0, e1)
 
-        warm = bank(7, [P, 2 * C], "warm")
-        for i in range(2):
-            nc.tensor.matmul_mx(
-                out=warm[:],
-                lhsT=slot_w[1].bitcast(FP8X4),
-                lhsT_scale=slot_plane[1],
-                rhs=groups[1][1][:].bitcast(FP8X4),
-                rhs_scale=groups[1][0][:],
-                start=True,
-                stop=True,
-            )
-
-        direct = len(DIRECT_GROUP)
         sorted_w, sorted_plane = {}, {}
-        for e in DIRECT_GROUP:
-            g, x = divmod(e, PLANE_ADAPTERS)
+        for e in DIRECT:
             sorted_w[e] = keep.tile([P, H], U16, name="sorted_w%d" % e, align_bytes=64)
             sorted_plane[e] = keep.tile([P, H], U8, name="sorted_plane%d" % e, align_bytes=64)
-            for dst, src in ((sorted_w[e], wa_w[g][:, x, :].bitcast(U16)), (sorted_plane[e], wa_planes[g][:, x, :])):
+            for dst, src in ((sorted_w[e], wa_w_of[e].bitcast(U16)), (sorted_plane[e], wa_plane_of[e])):
                 nc.gpsimd.tensor_copy(dst[:].rearrange("p (d m) -> p d m", d=4), src.rearrange("p (m d) -> p d m", d=4))
 
-        h_rows = {}
-
-        def first_layer(e, number):
-            sums = bank(number, [P, H], "h_sums%d" % e)
-            nc.tensor.matmul_mx(
-                out=sums[:],
-                lhsT=slot_w[e].bitcast(FP8X4),
-                lhsT_scale=slot_plane[e],
-                rhs=wa_w[e // PLANE_ADAPTERS][:, e % PLANE_ADAPTERS, :].bitcast(FP4X4),
-                rhs_scale=wa_planes[e // PLANE_ADAPTERS][:, e % PLANE_ADAPTERS, :],
-                start=True,
-                stop=True,
-            )
-            h_rows[e] = keep.tile([P, H], BF16, name="h_rows%d" % e, align_bytes=64)
-            dst = h_rows[e][:].rearrange("s (u p d) -> s u p d", u=2, d=2)
-            src = sums[:].rearrange("s (p u d) -> s u p d", u=2, d=2)
+        def relu(e, dst, src):
             if e in VECTOR_RELU:
                 nc.vector.tensor_scalar_max(dst, src, 0.0)
             else:
                 nc.scalar.activation(dst, src, RELU)
 
-        h_turned = {DIRECT_GROUP: keep.tile([P, direct * C * 4], BF16, name="h_direct", align_bytes=64)}
+        h_rows = {}
+
+        def turned_layer(e, number):
+            sums = bank(number, [P, H], "h_sums%d" % e)
+            nc.tensor.matmul_mx(
+                out=sums[:],
+                lhsT=slot_w[e].bitcast(FP8X4),
+                lhsT_scale=slot_plane[e],
+                rhs=wa_w_of[e].bitcast(FP4X4),
+                rhs_scale=wa_plane_of[e],
+                start=True,
+                stop=True,
+            )
+            h_rows[e] = keep.tile([P, H], BF16, name="h_rows%d" % e, align_bytes=64)
+            dst = h_rows[e][:].rearrange("s (u p d) -> s u p d", u=2, d=2)
+            relu(e, dst, sums[:].rearrange("s (p u d) -> s u p d", u=2, d=2))
+
+        h_ready = {DIRECT: keep.tile([P, len(DIRECT) * C * 4], BF16, name="h_direct", align_bytes=64)}
 
         def direct_layer(e, number):
             sums = bank(number, [P, 4, C], "h_sums%d" % e)
@@ -176,12 +160,9 @@ def tile_moe_adp_relu_kernel(
                     start=True,
                     stop=True,
                 )
-            dst = h_turned[DIRECT_GROUP][:, DIRECT_GROUP.index(e) * H : (DIRECT_GROUP.index(e) + 1) * H].rearrange("p (s d) -> p s d", d=4)
-            src = sums[:].rearrange("p d s -> p s d")
-            if e in VECTOR_RELU:
-                nc.vector.tensor_scalar_max(dst, src, 0.0)
-            else:
-                nc.scalar.activation(dst, src, RELU)
+            x = DIRECT.index(e)
+            dst = h_ready[DIRECT][:, x * C * 4 : (x + 1) * C * 4].rearrange("p (s d) -> p s d", d=4)
+            relu(e, dst, sums[:].rearrange("p d s -> p s d"))
 
         def turn(group, number, copy):
             count = len(group)
@@ -190,9 +171,9 @@ def tile_moe_adp_relu_kernel(
                 words = h_rows[e][:].bitcast(F32)
                 for u in range(2):
                     nc.tensor.transpose(pairs[:, x, u, :], words[:, u * P : (u + 1) * P], ident[:])
-            h_turned[group] = keep.tile([P, count * C * 4], BF16, name="h_turned%d" % group[0], align_bytes=64)
+            h_ready[group] = keep.tile([P, count * C * 4], BF16, name="h_turned%d" % group[0], align_bytes=64)
             copy(
-                h_turned[group][:].bitcast(F32).rearrange("p (x s u) -> p x s u", x=count, u=2),
+                h_ready[group][:].bitcast(F32).rearrange("p (x s u) -> p x s u", x=count, u=2),
                 pairs[:, 0:count, :, :].rearrange("p x u s -> p x s u"),
             )
 
@@ -217,7 +198,7 @@ def tile_moe_adp_relu_kernel(
         def quantize_and_multiply(group):
             words = keep.tile([P, len(group) * C], U32, name="h_w%d" % group[0], align_bytes=64)
             plane = keep.tile([P, len(group) * C], U8, name="h_plane%d" % group[0], align_bytes=64)
-            nc.vector.quantize_mx(out=words[:].bitcast(FP8X4), scales=plane[:], in_=h_turned[group][:])
+            nc.vector.quantize_mx(out=words[:].bitcast(FP8X4), scales=plane[:], in_=h_ready[group][:])
             for x, e in enumerate(group):
                 h_w[e] = words[:, x * C : (x + 1) * C]
                 h_plane[e] = plane[:, x * C : (x + 1) * C]
@@ -227,23 +208,23 @@ def tile_moe_adp_relu_kernel(
 
         def y_out(half, index, copy):
             members = Y_GROUPS[half][index][0]
-            chosen = slice(members[0], members[-1] + 1, members[1] - members[0] if len(members) > 1 else 1)
+            step = members[1] - members[0] if len(members) > 1 else 1
             copy(
-                y[half][:].rearrange("p (e c) -> p e c", c=C)[:, chosen, :],
+                y[half][:].rearrange("p (e c) -> p e c", c=C)[:, members[0] : members[-1] + 1 : step, :],
                 y_sums[(members, half)][:].rearrange("p (e c) -> p e c", c=C),
             )
 
         for e in range(1, E - 1):
-            first_layer(e, e - 1)
+            turned_layer(e, e - 1)
         turn((1, 2), 2, nc.vector.tensor_copy)
         turn((3, 4), 0, nc.scalar.copy)
         quantize_and_multiply((1, 2))
         direct_layer(0, 3)
-        direct_layer(7, 6)
+        direct_layer(E - 1, 6)
         quantize_and_multiply((3, 4))
-        turn((5,), 7, nc.scalar.copy)
+        turn((5,), BANKS - 1, nc.scalar.copy)
         turn((6,), 2, nc.scalar.copy)
-        quantize_and_multiply(DIRECT_GROUP)
+        quantize_and_multiply(DIRECT)
         quantize_and_multiply((5,))
         quantize_and_multiply((6,))
         y_out(0, 0, nc.scalar.copy)
@@ -252,7 +233,7 @@ def tile_moe_adp_relu_kernel(
         y_out(0, 3, nc.scalar.copy)
         second_layer(range(E), 1)
 
-        base_low_sums = bank(7, [P, T // P, P], "base_low_sums")
+        base_low_sums = bank(BANKS - 1, [P, T // P, P], "base_low_sums")
         for j in range(T // P):
             nc.tensor.matmul_mx(
                 out=base_low_sums[:, j, :],
@@ -291,7 +272,7 @@ def tile_moe_adp_relu_kernel(
                     sums, lhsT=term, rhs=ident[:], is_transpose=True, start=(i == 0), stop=(i == len(terms) - 1)
                 )
 
-        def finish_low(t0, first_bank, second_bank, queue):
+        def finish_low(t0, first_bank, second_bank):
             routed_sums = bank(first_bank, [P, 2, P], "routed_sums%d" % t0)
             for j in range(2):
                 tokens = slice(t0 + j * P, t0 + (j + 1) * P)
@@ -303,7 +284,7 @@ def tile_moe_adp_relu_kernel(
                 add_transposed(total[:, j, :], (base_low[:, t0 // P + j, :], routed[:, j, :]))
             result = keep.tile([P, 2 * P], F32, name="result_low%d" % t0)
             nc.scalar.copy(result[:], total[:].rearrange("p j t -> p (j t)"))
-            queue.dma_start(out=out[0:P, t0 : t0 + 2 * P], in_=result[:])
+            nc.scalar.dma_start(out=out[0:P, t0 : t0 + 2 * P], in_=result[:])
 
         def finish_high(t0, t1):
             result = keep.tile([P, t1 - t0], F32, name="result_high%d" % t0)
@@ -318,7 +299,7 @@ def tile_moe_adp_relu_kernel(
         fetch(1, 1, 0, LAST_STORE)
         nc.vector.tensor_tensor(partial_high[:], base_high[:], gated[0][1][:], ADD)
         fetch(1, 1, LAST_STORE, T)
-        finish_low(0, 1, 4, nc.scalar)
-        finish_low(middle, 5, 6, nc.scalar)
+        finish_low(0, 1, 4)
+        finish_low(middle, 5, 6)
         finish_high(0, LAST_STORE)
         finish_high(LAST_STORE, T)

@@ -15,6 +15,7 @@ U16 = mybir.dt.uint16
 U8 = mybir.dt.uint8
 FP8X4 = mybir.dt.float8_e4m3fn_x4
 FP4X4 = mybir.dt.float4_e2m1fn_x4
+COPY = mybir.ActivationFunctionType.Copy
 MULT = mybir.AluOpType.mult
 ADD = mybir.AluOpType.add
 RELU = mybir.ActivationFunctionType.Relu
@@ -26,8 +27,9 @@ LOAD_ADAPTERS = 4
 DIRECT = (0, E - 1)
 GATHER_GROUPS = [(1, 3), (3, 6), (6, E), (0, 1)]
 VECTOR_RELU = (5, 0)
-Y_GROUPS = [[((1, 2, 3, 4), 1), (DIRECT, 4), ((5,), 5), ((6,), 6)], [((0, 1, 2, 3), 2), ((4, 5, 6, 7), 3)]]
-LAST_STORE = 320
+Y_GROUPS = [[((1, 2, 3, 4), 1), (DIRECT, 4), ((5,), 5), ((6,), 6)], [((1, 2, 3, 4), 7), (DIRECT, 3), ((5, 6), 2)]]
+TURNED_BLOCKS = 3
+BLOCKS = T // P
 
 
 def load_scale_rows(queues, plane, rows):
@@ -68,7 +70,9 @@ def tile_moe_adp_relu_kernel(
         wa_planes = [keep.tile([P, LOAD_ADAPTERS, H], U8, name="wa_plane%d" % g, align_bytes=64) for g in wa_loads]
         wb_plane = keep.tile([P, E, N], U8, name="wb_plane", align_bytes=64)
         wb_w = keep.tile([P, E, 2 * N], U8, name="wb_w", align_bytes=64)
-        gate_t = keep.tile([P, 2, T], F32, name="gate_t")
+        gate_rows = keep.tile([P, T], F32, name="gate_rows")
+        gate_last = keep.tile([P, P], F32, name="gate_last")
+        gate_columns = keep.tile([P, TURNED_BLOCKS], F32, name="gate_columns")
         ident = keep.tile([P, P], F32, name="ident")
         wa_w = [keep.tile([P, LOAD_ADAPTERS, 2 * H], U8, name="wa_w%d" % g, align_bytes=64) for g in wa_loads]
         wa_w_of = [wa_w[e // LOAD_ADAPTERS][:, e % LOAD_ADAPTERS, :] for e in range(E)]
@@ -95,13 +99,16 @@ def tile_moe_adp_relu_kernel(
         load_wa_plane(0)
         load_wa_words(1, nc.sync)
         load_wa_plane(1)
-        nc.sync.dma_start(out=wb_w[:].bitcast(I32), in_=wb_words[:, 0].rearrange("e p c -> p e c").bitcast(I32))
-        load_scale_rows(sync_queue, wb_plane, wb_scales[:, 0])
         nc.sync.dma_start(out=w_w[:].bitcast(I32), in_=w_words[0].rearrange("p n d -> p (n d)").bitcast(I32))
         fill_scale_plane(sync_queue, w_plane, w_scales[0])
+        nc.sync.dma_start(out=wb_w[:].bitcast(I32), in_=wb_words[:, 0].rearrange("e p c -> p e c").bitcast(I32))
+        load_scale_rows(sync_queue, wb_plane, wb_scales[:, 0])
         nc.sync.dma_start(pos_t[0][:], pos1)
         nc.sync.dma_start(pos_t[1][:], pos2)
-        nc.sync.dma_start(out=gate_t[:], in_=gate.rearrange("r p t -> p r t"))
+        with nc.allow_non_contiguous_dma(reason="one gate value a partition"):
+            nc.sync.dma_start(out=gate_columns[:], in_=gate[0, 0, 0 : TURNED_BLOCKS * P].rearrange("(j p) -> p j", p=P))
+        nc.sync.dma_start(out=gate_rows[:], in_=gate[1])
+        nc.sync.dma_start(out=gate_last[:], in_=gate[0, :, TURNED_BLOCKS * P : T])
 
         slot_w, slot_plane = {}, {}
 
@@ -224,6 +231,20 @@ def tile_moe_adp_relu_kernel(
         quantize_and_multiply((3, 4))
         turn((5,), BANKS - 1, nc.scalar.copy)
         turn((6,), 2, nc.scalar.copy)
+        def frozen(sums, tokens, rows, token_major):
+            a = (x_w[:, tokens].bitcast(FP8X4), x_plane[:, tokens])
+            b = (w_w[:, rows].bitcast(FP8X4), w_plane[:, rows])
+            lhs, rhs = (a, b) if token_major else (b, a)
+            nc.tensor.matmul_mx(out=sums, lhsT=lhs[0], lhsT_scale=lhs[1], rhs=rhs[0], rhs_scale=rhs[1], start=True, stop=True)
+
+        blocks = [slice(j * P, (j + 1) * P) for j in range(BLOCKS)]
+        base_t = keep.tile([P, TURNED_BLOCKS, N], F32, name="base_t")
+        base_a = bank(0, [P, 2, N], "base_a")
+        frozen(base_a[:, 0, :], blocks[0], slice(0, N), True)
+        for half in range(2):
+            frozen(base_a[:, 1, half * P : (half + 1) * P], blocks[BLOCKS - 1], slice(half * P, (half + 1) * P), False)
+        nc.scalar.copy(base_t[:, 0, :], base_a[:, 0, :])
+        second_layer((1, 2, 3, 4), 1)
         quantize_and_multiply(DIRECT)
         quantize_and_multiply((5,))
         quantize_and_multiply((6,))
@@ -231,75 +252,58 @@ def tile_moe_adp_relu_kernel(
         y_out(0, 1, nc.vector.tensor_copy)
         y_out(0, 2, nc.scalar.copy)
         y_out(0, 3, nc.scalar.copy)
-        second_layer(range(E), 1)
+        y_out(1, 0, nc.vector.tensor_copy)
+        second_layer(DIRECT + (5, 6), 1)
+        y_out(1, 1, nc.vector.tensor_copy)
+        y_out(1, 2, nc.scalar.copy)
+        base_b = bank(1, [P, 2, N], "base_b")
+        for j in (1, 2):
+            frozen(base_b[:, j - 1, :], blocks[j], slice(0, N), True)
 
-        base_low_sums = bank(BANKS - 1, [P, T // P, P], "base_low_sums")
-        for j in range(T // P):
-            nc.tensor.matmul_mx(
-                out=base_low_sums[:, j, :],
-                lhsT=x_w[:, j * P : (j + 1) * P].bitcast(FP8X4),
-                lhsT_scale=x_plane[:, j * P : (j + 1) * P],
-                rhs=w_w[:, 0:P].bitcast(FP8X4),
-                rhs_scale=w_plane[:, 0:P],
-                start=True,
-                stop=True,
-            )
-        base_high = bank(0, [P, T], "base_high")
-        nc.tensor.matmul_mx(
-            out=base_high[:],
-            lhsT=w_w[:, P:N].bitcast(FP8X4),
-            lhsT_scale=w_plane[:, P:N],
-            rhs=x_w[:].bitcast(FP8X4),
-            rhs_scale=x_plane[:],
-            start=True,
-            stop=True,
-        )
-        y_out(1, 0, nc.scalar.copy)
-        y_out(1, 1, nc.scalar.copy)
+        turned_tokens = TURNED_BLOCKS * P
+        first_low = keep.tile([P, turned_tokens], F32, name="first_low")
+        first_high = [keep.tile([P, P], F32, name="first_high%d" % j) for j in range(TURNED_BLOCKS)]
+        first_last = keep.tile([P, 2, P], F32, name="first_last")
+        second = keep.tile([P, 2, T], F32, name="second")
+        cut = turned_tokens // LIST_COLUMN
+        nc.scalar.activation(first_low[:], y[0][:].indirect(pos_t[0][:, 0:cut]), COPY)
+        nc.scalar.copy(base_t[:, 1:3, :], base_b[:])
+        step = P // LIST_COLUMN
+        for j in range(TURNED_BLOCKS):
+            nc.scalar.activation(first_high[j][:], y[1][:].indirect(pos_t[0][:, j * step : (j + 1) * step]), COPY)
+        for half in range(2):
+            nc.vector.tensor_tensor(second[:, half, :], y[half][:].indirect(pos_t[1][:]), gate_rows[:], MULT)
 
-        gated = [[keep.tile([P, T], F32, name="gated%d_%d" % (r, half)) for half in range(2)] for r in range(2)]
-        partial_high = keep.tile([P, T], F32, name="partial_high")
-        base_low = keep.tile([P, T // P, P], F32, name="base_low")
-        nc.scalar.copy(base_low[:], base_low_sums[:])
+        def transpose(dst, src, start, stop):
+            nc.tensor.matmul(dst, lhsT=src, rhs=ident[:], is_transpose=True, start=start, stop=stop)
 
-        def fetch(r, half, t0, t1):
-            entries = pos_t[r][:, t0 // LIST_COLUMN : t1 // LIST_COLUMN]
-            nc.vector.tensor_tensor(gated[r][half][:, t0:t1], y[half][:].indirect(entries), gate_t[:, r, t0:t1], MULT)
+        def store(j, result):
+            nc.sync.dma_start(out=out[:, blocks[j]].rearrange("(h n) t -> n h t", h=2), in_=result[:])
 
-        def add_transposed(sums, terms):
-            for i, term in enumerate(terms):
-                nc.tensor.matmul(
-                    sums, lhsT=term, rhs=ident[:], is_transpose=True, start=(i == 0), stop=(i == len(terms) - 1)
-                )
-
-        def finish_low(t0, first_bank, second_bank):
-            routed_sums = bank(first_bank, [P, 2, P], "routed_sums%d" % t0)
-            for j in range(2):
-                tokens = slice(t0 + j * P, t0 + (j + 1) * P)
-                add_transposed(routed_sums[:, j, :], (gated[0][0][:, tokens], gated[1][0][:, tokens]))
-            routed = keep.tile([P, 2, P], F32, name="routed%d" % t0)
-            nc.scalar.copy(routed[:], routed_sums[:])
-            total = bank(second_bank, [P, 2, P], "total%d" % t0)
-            for j in range(2):
-                add_transposed(total[:, j, :], (base_low[:, t0 // P + j, :], routed[:, j, :]))
-            result = keep.tile([P, 2 * P], F32, name="result_low%d" % t0)
-            nc.scalar.copy(result[:], total[:].rearrange("p j t -> p (j t)"))
-            nc.scalar.dma_start(out=out[0:P, t0 : t0 + 2 * P], in_=result[:])
-
-        def finish_high(t0, t1):
-            result = keep.tile([P, t1 - t0], F32, name="result_high%d" % t0)
-            nc.vector.tensor_tensor(result[:], partial_high[:, t0:t1], gated[1][1][:, t0:t1], ADD)
-            nc.sync.dma_start(out=out[P:N, t0:t1], in_=result[:])
-
-        middle = T // 2
-        fetch(0, 0, 0, T)
-        for t0 in (0, middle):
-            fetch(1, 0, t0, t0 + middle)
-        fetch(0, 1, 0, T)
-        fetch(1, 1, 0, LAST_STORE)
-        nc.vector.tensor_tensor(partial_high[:], base_high[:], gated[0][1][:], ADD)
-        fetch(1, 1, LAST_STORE, T)
-        finish_low(0, 1, 4)
-        finish_low(middle, 5, 6)
-        finish_high(0, LAST_STORE)
-        finish_high(LAST_STORE, T)
+        turned = [bank((7, 3, 2)[j], [P, 2, P], "turned%d" % j) for j in range(TURNED_BLOCKS)]
+        totals = [bank((4, 5, 6)[j], [P, 2, P], "total%d" % j) for j in range(TURNED_BLOCKS)]
+        for j in range(TURNED_BLOCKS):
+            transpose(turned[j][:, 0, :], first_low[:, blocks[j]], True, True)
+        for j in range(TURNED_BLOCKS):
+            for half in range(2):
+                transpose(totals[j][:, half, :], base_t[:, j, half * P : (half + 1) * P], half == 0, False)
+        for j in range(TURNED_BLOCKS):
+            transpose(turned[j][:, 1, :], first_high[j][:], True, True)
+        last = BLOCKS - 1
+        partial = keep.tile([P, 2, P], F32, name="partial")
+        nc.vector.tensor_tensor(partial[:], base_a[:, 1, :].rearrange("p (h t) -> p h t", h=2), second[:, :, blocks[last]], ADD)
+        for half in range(2):
+            entries = pos_t[0][:, cut : T // LIST_COLUMN]
+            nc.vector.tensor_tensor(first_last[:, half, :], y[half][:].indirect(entries), gate_last[:], MULT)
+        for j in range(TURNED_BLOCKS):
+            gated = keep.tile([P, N], F32, name="gated%d" % j)
+            nc.scalar.activation(gated[:], turned[j][:].rearrange("p h n -> p (h n)"), COPY, scale=gate_columns[:, j : j + 1])
+            for half in range(2):
+                transpose(totals[j][:, half, :], gated[:, half * P : (half + 1) * P], False, half == 1)
+        result = keep.tile([P, 2, P], F32, name="result_last")
+        nc.vector.tensor_tensor(result[:], partial[:], first_last[:], ADD)
+        store(last, result)
+        for j in range(TURNED_BLOCKS):
+            result = keep.tile([P, 2, P], F32, name="result%d" % j)
+            nc.vector.tensor_tensor(result[:], totals[j][:], second[:, :, blocks[j]], ADD)
+            store(j, result)

@@ -70,8 +70,7 @@ def tile_moe_adp_relu_kernel(
         wa_planes = [keep.tile([P, LOAD_ADAPTERS, H], U8, name="wa_plane%d" % g, align_bytes=64) for g in wa_loads]
         wb_plane = keep.tile([P, E, N], U8, name="wb_plane", align_bytes=64)
         wb_w = keep.tile([P, E, 2 * N], U8, name="wb_w", align_bytes=64)
-        gate_rows = keep.tile([P, T], F32, name="gate_rows")
-        gate_last = keep.tile([P, P], F32, name="gate_last")
+        gate_t = keep.tile([P, 2, T], F32, name="gate_t")
         gate_columns = keep.tile([P, TURNED_BLOCKS], F32, name="gate_columns")
         ident = keep.tile([P, P], F32, name="ident")
         wa_w = [keep.tile([P, LOAD_ADAPTERS, 2 * H], U8, name="wa_w%d" % g, align_bytes=64) for g in wa_loads]
@@ -105,10 +104,7 @@ def tile_moe_adp_relu_kernel(
         load_scale_rows(sync_queue, wb_plane, wb_scales[:, 0])
         nc.sync.dma_start(pos_t[0][:], pos1)
         nc.sync.dma_start(pos_t[1][:], pos2)
-        with nc.allow_non_contiguous_dma(reason="one gate value a partition"):
-            nc.sync.dma_start(out=gate_columns[:], in_=gate[0, 0, 0 : TURNED_BLOCKS * P].rearrange("(j p) -> p j", p=P))
-        nc.sync.dma_start(out=gate_rows[:], in_=gate[1])
-        nc.sync.dma_start(out=gate_last[:], in_=gate[0, :, TURNED_BLOCKS * P : T])
+        nc.sync.dma_start(out=gate_t[:], in_=gate.rearrange("r p t -> p r t"))
 
         slot_w, slot_plane = {}, {}
 
@@ -238,12 +234,12 @@ def tile_moe_adp_relu_kernel(
             nc.tensor.matmul_mx(out=sums, lhsT=lhs[0], lhsT_scale=lhs[1], rhs=rhs[0], rhs_scale=rhs[1], start=True, stop=True)
 
         blocks = [slice(j * P, (j + 1) * P) for j in range(BLOCKS)]
-        base_t = keep.tile([P, TURNED_BLOCKS, N], F32, name="base_t")
+        base_first = keep.tile([P, N], F32, name="base_first")
         base_a = bank(0, [P, 2, N], "base_a")
         frozen(base_a[:, 0, :], blocks[0], slice(0, N), True)
         for half in range(2):
             frozen(base_a[:, 1, half * P : (half + 1) * P], blocks[BLOCKS - 1], slice(half * P, (half + 1) * P), False)
-        nc.scalar.copy(base_t[:, 0, :], base_a[:, 0, :])
+        nc.scalar.copy(base_first[:], base_a[:, 0, :])
         second_layer((1, 2, 3, 4), 1)
         quantize_and_multiply(DIRECT)
         quantize_and_multiply((5,))
@@ -261,18 +257,17 @@ def tile_moe_adp_relu_kernel(
             frozen(base_b[:, j - 1, :], blocks[j], slice(0, N), True)
 
         turned_tokens = TURNED_BLOCKS * P
-        first_low = keep.tile([P, turned_tokens], F32, name="first_low")
+        first_low = keep.tile([P, turned_tokens], F32, name="first_low", tag="low_then_base")
         first_high = [keep.tile([P, P], F32, name="first_high%d" % j) for j in range(TURNED_BLOCKS)]
         first_last = keep.tile([P, 2, P], F32, name="first_last")
         second = keep.tile([P, 2, T], F32, name="second")
         cut = turned_tokens // LIST_COLUMN
         nc.scalar.activation(first_low[:], y[0][:].indirect(pos_t[0][:, 0:cut]), COPY)
-        nc.scalar.copy(base_t[:, 1:3, :], base_b[:])
         step = P // LIST_COLUMN
         for j in range(TURNED_BLOCKS):
             nc.scalar.activation(first_high[j][:], y[1][:].indirect(pos_t[0][:, j * step : (j + 1) * step]), COPY)
         for half in range(2):
-            nc.vector.tensor_tensor(second[:, half, :], y[half][:].indirect(pos_t[1][:]), gate_rows[:], MULT)
+            nc.vector.tensor_tensor(second[:, half, :], y[half][:].indirect(pos_t[1][:]), gate_t[:, 1, :], MULT)
 
         def transpose(dst, src, start, stop):
             nc.tensor.matmul(dst, lhsT=src, rhs=ident[:], is_transpose=True, start=start, stop=stop)
@@ -280,21 +275,28 @@ def tile_moe_adp_relu_kernel(
         def store(j, result):
             nc.sync.dma_start(out=out[:, blocks[j]].rearrange("(h n) t -> n h t", h=2), in_=result[:])
 
+        gate_turned = bank(5, [P, TURNED_BLOCKS, P], "gate_turned")
+        for j in range(TURNED_BLOCKS):
+            transpose(gate_turned[:, j, :], gate_t[:, 0, blocks[j]], True, True)
+        nc.scalar.copy(gate_columns[:], gate_turned[:, :, 0])
         turned = [bank((7, 3, 2)[j], [P, 2, P], "turned%d" % j) for j in range(TURNED_BLOCKS)]
         totals = [bank((4, 5, 6)[j], [P, 2, P], "total%d" % j) for j in range(TURNED_BLOCKS)]
         for j in range(TURNED_BLOCKS):
             transpose(turned[j][:, 0, :], first_low[:, blocks[j]], True, True)
         for j in range(TURNED_BLOCKS):
-            for half in range(2):
-                transpose(totals[j][:, half, :], base_t[:, j, half * P : (half + 1) * P], half == 0, False)
-        for j in range(TURNED_BLOCKS):
             transpose(turned[j][:, 1, :], first_high[j][:], True, True)
+        base_rest = keep.tile([P, 2, N], F32, name="base_rest", tag="low_then_base")
+        nc.scalar.copy(base_rest[:], base_b[:])
+        base_t = [base_first[:], base_rest[:, 0, :], base_rest[:, 1, :]]
+        for j in range(TURNED_BLOCKS):
+            for half in range(2):
+                transpose(totals[j][:, half, :], base_t[j][:, half * P : (half + 1) * P], half == 0, False)
         last = BLOCKS - 1
         partial = keep.tile([P, 2, P], F32, name="partial")
         nc.vector.tensor_tensor(partial[:], base_a[:, 1, :].rearrange("p (h t) -> p h t", h=2), second[:, :, blocks[last]], ADD)
         for half in range(2):
             entries = pos_t[0][:, cut : T // LIST_COLUMN]
-            nc.vector.tensor_tensor(first_last[:, half, :], y[half][:].indirect(entries), gate_last[:], MULT)
+            nc.vector.tensor_tensor(first_last[:, half, :], y[half][:].indirect(entries), gate_t[:, 0, blocks[last]], MULT)
         for j in range(TURNED_BLOCKS):
             gated = keep.tile([P, N], F32, name="gated%d" % j)
             nc.scalar.activation(gated[:], turned[j][:].rearrange("p h n -> p (h n)"), COPY, scale=gate_columns[:, j : j + 1])

@@ -27,9 +27,8 @@ LOAD_ADAPTERS = 4
 DIRECT = (0, E - 1)
 GATHER_GROUPS = [(1, 3), (3, 6), (6, E), (0, 1)]
 VECTOR_RELU = (5, 0)
-Y_GROUPS = [[((1, 2, 3, 4), 1), (DIRECT, 4), ((5,), 5), ((6,), 6)], [((1, 2, 3, 4), 7), (DIRECT, 3), ((5, 6), 2)]]
-TURNED_BLOCKS = 3
-BLOCKS = T // P
+Y_GROUPS = [[((1, 2, 3, 4), 1), (DIRECT, 4), ((5,), 5), ((6,), 6)], [((0, 1, 2, 3), 2), ((4, 5, 6, 7), 3)]]
+TURNED = 2 * P
 
 
 def load_scale_rows(queues, plane, rows):
@@ -71,7 +70,6 @@ def tile_moe_adp_relu_kernel(
         wb_plane = keep.tile([P, E, N], U8, name="wb_plane", align_bytes=64)
         wb_w = keep.tile([P, E, 2 * N], U8, name="wb_w", align_bytes=64)
         gate_t = keep.tile([P, 2, T], F32, name="gate_t")
-        gate_columns = keep.tile([P, TURNED_BLOCKS], F32, name="gate_columns")
         ident = keep.tile([P, P], F32, name="ident")
         wa_w = [keep.tile([P, LOAD_ADAPTERS, 2 * H], U8, name="wa_w%d" % g, align_bytes=64) for g in wa_loads]
         wa_w_of = [wa_w[e // LOAD_ADAPTERS][:, e % LOAD_ADAPTERS, :] for e in range(E)]
@@ -98,13 +96,13 @@ def tile_moe_adp_relu_kernel(
         load_wa_plane(0)
         load_wa_words(1, nc.sync)
         load_wa_plane(1)
-        nc.sync.dma_start(out=w_w[:].bitcast(I32), in_=w_words[0].rearrange("p n d -> p (n d)").bitcast(I32))
-        fill_scale_plane(sync_queue, w_plane, w_scales[0])
         nc.sync.dma_start(out=wb_w[:].bitcast(I32), in_=wb_words[:, 0].rearrange("e p c -> p e c").bitcast(I32))
         load_scale_rows(sync_queue, wb_plane, wb_scales[:, 0])
-        nc.sync.dma_start(pos_t[0][:], pos1)
-        nc.sync.dma_start(pos_t[1][:], pos2)
+        nc.sync.dma_start(out=w_w[:].bitcast(I32), in_=w_words[0].rearrange("p n d -> p (n d)").bitcast(I32))
+        fill_scale_plane(sync_queue, w_plane, w_scales[0])
         nc.sync.dma_start(out=gate_t[:], in_=gate.rearrange("r p t -> p r t"))
+        nc.sync.dma_start(pos_t[1][:], pos2)
+        nc.sync.dma_start(pos_t[0][:], pos1)
 
         slot_w, slot_plane = {}, {}
 
@@ -227,20 +225,6 @@ def tile_moe_adp_relu_kernel(
         quantize_and_multiply((3, 4))
         turn((5,), BANKS - 1, nc.scalar.copy)
         turn((6,), 2, nc.scalar.copy)
-        def frozen(sums, tokens, rows, token_major):
-            a = (x_w[:, tokens].bitcast(FP8X4), x_plane[:, tokens])
-            b = (w_w[:, rows].bitcast(FP8X4), w_plane[:, rows])
-            lhs, rhs = (a, b) if token_major else (b, a)
-            nc.tensor.matmul_mx(out=sums, lhsT=lhs[0], lhsT_scale=lhs[1], rhs=rhs[0], rhs_scale=rhs[1], start=True, stop=True)
-
-        blocks = [slice(j * P, (j + 1) * P) for j in range(BLOCKS)]
-        base_first = keep.tile([P, N], F32, name="base_first")
-        base_a = bank(0, [P, 2, N], "base_a")
-        frozen(base_a[:, 0, :], blocks[0], slice(0, N), True)
-        for half in range(2):
-            frozen(base_a[:, 1, half * P : (half + 1) * P], blocks[BLOCKS - 1], slice(half * P, (half + 1) * P), False)
-        nc.scalar.copy(base_first[:], base_a[:, 0, :])
-        second_layer((1, 2, 3, 4), 1)
         quantize_and_multiply(DIRECT)
         quantize_and_multiply((5,))
         quantize_and_multiply((6,))
@@ -248,64 +232,71 @@ def tile_moe_adp_relu_kernel(
         y_out(0, 1, nc.vector.tensor_copy)
         y_out(0, 2, nc.scalar.copy)
         y_out(0, 3, nc.scalar.copy)
-        y_out(1, 0, nc.vector.tensor_copy)
-        second_layer(DIRECT + (5, 6), 1)
-        y_out(1, 1, nc.vector.tensor_copy)
-        y_out(1, 2, nc.scalar.copy)
-        base_b = bank(1, [P, 2, N], "base_b")
-        for j in (1, 2):
-            frozen(base_b[:, j - 1, :], blocks[j], slice(0, N), True)
+        second_layer(range(E), 1)
 
-        turned_tokens = TURNED_BLOCKS * P
-        first_low = keep.tile([P, turned_tokens], F32, name="first_low", tag="low_then_base")
-        first_high = [keep.tile([P, P], F32, name="first_high%d" % j) for j in range(TURNED_BLOCKS)]
-        first_last = keep.tile([P, 2, P], F32, name="first_last")
-        second = keep.tile([P, 2, T], F32, name="second")
-        cut = turned_tokens // LIST_COLUMN
-        nc.scalar.activation(first_low[:], y[0][:].indirect(pos_t[0][:, 0:cut]), COPY)
-        step = P // LIST_COLUMN
-        for j in range(TURNED_BLOCKS):
-            nc.scalar.activation(first_high[j][:], y[1][:].indirect(pos_t[0][:, j * step : (j + 1) * step]), COPY)
-        for half in range(2):
-            nc.vector.tensor_tensor(second[:, half, :], y[half][:].indirect(pos_t[1][:]), gate_t[:, 1, :], MULT)
+        def frozen(sums, tokens, rows, token_major):
+            a = (x_w[:, tokens].bitcast(FP8X4), x_plane[:, tokens])
+            b = (w_w[:, rows].bitcast(FP8X4), w_plane[:, rows])
+            lhs, rhs = (a, b) if token_major else (b, a)
+            nc.tensor.matmul_mx(out=sums, lhsT=lhs[0], lhsT_scale=lhs[1], rhs=rhs[0], rhs_scale=rhs[1], start=True, stop=True)
 
         def transpose(dst, src, start, stop):
             nc.tensor.matmul(dst, lhsT=src, rhs=ident[:], is_transpose=True, start=start, stop=stop)
 
-        def store(j, result):
-            nc.sync.dma_start(out=out[:, blocks[j]].rearrange("(h n) t -> n h t", h=2), in_=result[:])
-
-        gate_turned = bank(5, [P, TURNED_BLOCKS, P], "gate_turned")
-        for j in range(TURNED_BLOCKS):
-            transpose(gate_turned[:, j, :], gate_t[:, 0, blocks[j]], True, True)
-        nc.scalar.copy(gate_columns[:], gate_turned[:, :, 0])
-        turned = [bank((7, 3, 2)[j], [P, 2, P], "turned%d" % j) for j in range(TURNED_BLOCKS)]
-        totals = [bank((4, 5, 6)[j], [P, 2, P], "total%d" % j) for j in range(TURNED_BLOCKS)]
-        for j in range(TURNED_BLOCKS):
-            transpose(turned[j][:, 0, :], first_low[:, blocks[j]], True, True)
-        for j in range(TURNED_BLOCKS):
-            transpose(turned[j][:, 1, :], first_high[j][:], True, True)
-        base_rest = keep.tile([P, 2, N], F32, name="base_rest", tag="low_then_base")
-        nc.scalar.copy(base_rest[:], base_b[:])
-        base_t = [base_first[:], base_rest[:, 0, :], base_rest[:, 1, :]]
-        for j in range(TURNED_BLOCKS):
-            for half in range(2):
-                transpose(totals[j][:, half, :], base_t[j][:, half * P : (half + 1) * P], half == 0, False)
-        last = BLOCKS - 1
-        partial = keep.tile([P, 2, P], F32, name="partial")
-        nc.vector.tensor_tensor(partial[:], base_a[:, 1, :].rearrange("p (h t) -> p h t", h=2), second[:, :, blocks[last]], ADD)
+        blocks = [slice(j * P, (j + 1) * P) for j in range(TURNED // P)]
+        halves = [slice(half * P, (half + 1) * P) for half in range(2)]
+        rest = slice(TURNED, T)
+        base_turned = bank(BANKS - 1, [P, 2, N], "base_turned")
+        for j in range(2):
+            frozen(base_turned[:, j, :], blocks[j], slice(0, N), True)
+        base_rest = bank(0, [P, 2, T - TURNED], "base_rest")
         for half in range(2):
-            entries = pos_t[0][:, cut : T // LIST_COLUMN]
-            nc.vector.tensor_tensor(first_last[:, half, :], y[half][:].indirect(entries), gate_t[:, 0, blocks[last]], MULT)
-        for j in range(TURNED_BLOCKS):
+            frozen(base_rest[:, half, :], rest, halves[half], False)
+        y_out(1, 0, nc.scalar.copy)
+        y_out(1, 1, nc.scalar.copy)
+
+        step = P // LIST_COLUMN
+        first_low = keep.tile([P, TURNED], F32, name="first_low", tag="low_then_base")
+        first_high = [keep.tile([P, P], F32, name="first_high%d" % j) for j in range(2)]
+        first_rest = keep.tile([P, 2, T - TURNED], F32, name="first_rest")
+        second = keep.tile([P, 2, T], F32, name="second")
+        nc.scalar.activation(first_low[:], y[0][:].indirect(pos_t[0][:, 0 : 2 * step]), COPY)
+        for j in range(2):
+            nc.scalar.activation(first_high[j][:], y[1][:].indirect(pos_t[0][:, j * step : (j + 1) * step]), COPY)
+        for half in range(2):
+            nc.vector.tensor_tensor(second[:, half, :], y[half][:].indirect(pos_t[1][:]), gate_t[:, 1, :], MULT)
+            entries = pos_t[0][:, 2 * step : T // LIST_COLUMN]
+            nc.vector.tensor_tensor(first_rest[:, half, :], y[half][:].indirect(entries), gate_t[:, 0, rest], MULT)
+
+        gate_turned = bank(1, [P, 2, P], "gate_turned")
+        for j in range(2):
+            transpose(gate_turned[:, j, :], gate_t[:, 0, blocks[j]], True, True)
+        turned = [bank((4, 5)[j], [P, 2, P], "turned%d" % j) for j in range(2)]
+        for j in range(2):
+            transpose(turned[j][:, 0, :], first_low[:, blocks[j]], True, True)
+        for j in range(2):
+            transpose(turned[j][:, 1, :], first_high[j][:], True, True)
+        base_t = keep.tile([P, 2, N], F32, name="base_t", tag="low_then_base")
+        nc.scalar.copy(base_t[:], base_turned[:])
+        gate_columns = keep.tile([P, 2], F32, name="gate_columns")
+        nc.scalar.copy(gate_columns[:], gate_turned[:, :, 0])
+        totals = [bank((6, 2)[half], [P, 2, P], "total%d" % half) for half in range(2)]
+        for half in range(2):
+            for j in range(2):
+                transpose(totals[half][:, j, :], base_t[:, j, halves[half]], j == 0, False)
+        for j in range(2):
             gated = keep.tile([P, N], F32, name="gated%d" % j)
             nc.scalar.activation(gated[:], turned[j][:].rearrange("p h n -> p (h n)"), COPY, scale=gate_columns[:, j : j + 1])
             for half in range(2):
-                transpose(totals[j][:, half, :], gated[:, half * P : (half + 1) * P], False, half == 1)
-        result = keep.tile([P, 2, P], F32, name="result_last")
-        nc.vector.tensor_tensor(result[:], partial[:], first_last[:], ADD)
-        store(last, result)
-        for j in range(TURNED_BLOCKS):
-            result = keep.tile([P, 2, P], F32, name="result%d" % j)
-            nc.vector.tensor_tensor(result[:], totals[j][:], second[:, :, blocks[j]], ADD)
-            store(j, result)
+                transpose(totals[half][:, j, :], gated[:, halves[half]], False, j == 1)
+
+        partial = keep.tile([P, 2, T - TURNED], F32, name="partial")
+        nc.vector.tensor_tensor(partial[:], base_rest[:], second[:, :, rest], ADD)
+        for half in range(2):
+            result = keep.tile([P, T - TURNED], F32, name="result_rest%d" % half)
+            nc.vector.tensor_tensor(result[:], partial[:, half, :], first_rest[:, half, :], ADD)
+            nc.sync.dma_start(out=out[halves[half], rest], in_=result[:])
+        for half in range(2):
+            result = keep.tile([P, TURNED], F32, name="result_turned%d" % half)
+            nc.vector.tensor_tensor(result[:], totals[half][:].rearrange("p j t -> p (j t)"), second[:, half, 0:TURNED], ADD)
+            nc.sync.dma_start(out=out[halves[half], 0:TURNED], in_=result[:])

@@ -263,10 +263,24 @@ def tile_moe_adp_relu_kernel(
         nc.scalar.activation(first_low[:], y[0][:].indirect(pos_t[0][:, 0 : 2 * step]), COPY)
         for j in range(2):
             nc.scalar.activation(first_high[j][:], y[1][:].indirect(pos_t[0][:, j * step : (j + 1) * step]), COPY)
-        for half in range(2):
+        partial = keep.tile([P, 2, T - TURNED], F32, name="partial")
+
+        def fetch_second(half):
             nc.vector.tensor_tensor(second[:, half, :], y[half][:].indirect(pos_t[1][:]), gate_t[:, 1, :], MULT)
+
+        def fetch_first(half):
             entries = pos_t[0][:, 2 * step : T // LIST_COLUMN]
             nc.vector.tensor_tensor(first_rest[:, half, :], y[half][:].indirect(entries), gate_t[:, 0, rest], MULT)
+
+        def add_base(half):
+            nc.vector.tensor_tensor(partial[:, half, :], base_rest[:, half, :], second[:, half, rest], ADD)
+
+        fetch_second(0)
+        fetch_first(0)
+        fetch_second(1)
+        add_base(0)
+        fetch_first(1)
+        add_base(1)
 
         gate_turned = bank(1, [P, 2, P], "gate_turned")
         for j in range(2):
@@ -290,8 +304,6 @@ def tile_moe_adp_relu_kernel(
             for half in range(2):
                 transpose(totals[half][:, j, :], gated[:, halves[half]], False, j == 1)
 
-        partial = keep.tile([P, 2, T - TURNED], F32, name="partial")
-        nc.vector.tensor_tensor(partial[:], base_rest[:], second[:, :, rest], ADD)
         for half in range(2):
             result = keep.tile([P, T - TURNED], F32, name="result_rest%d" % half)
             nc.vector.tensor_tensor(result[:], partial[:, half, :], first_rest[:, half, :], ADD)

from contextlib import ExitStack

import concourse.mybir as mybir
from concourse.masks import make_identity

K, T, E, C, H, N = 512, 512, 8, 128, 512, 256
SLOTS = E * C
FLOPS = 2 * K * N * T + 2 * K * H * SLOTS + 2 * H * N * SLOTS

F32 = mybir.dt.float32
BF16 = mybir.dt.bfloat16
I32 = mybir.dt.int32
U32 = mybir.dt.uint32
U16 = mybir.dt.uint16
U8 = mybir.dt.uint8
FP8X4 = mybir.dt.float8_e4m3fn_x4
FP4X4 = mybir.dt.float4_e2m1fn_x4
COPY = mybir.ActivationFunctionType.Copy
MULT = mybir.AluOpType.mult
ADD = mybir.AluOpType.add
RELU = mybir.ActivationFunctionType.Relu

P = 128
LIST_COLUMN = 16
BANKS = 8
LOAD_ADAPTERS = 4
DIRECT = (0, E - 1)
GATHER_GROUPS = [(1, 3), (3, 6), (6, E), (0, 1)]
VECTOR_RELU = (5, 0)
Y_GROUPS = [[((1, 2, 3, 4), 1), (DIRECT, 4), ((5,), 5), ((6,), 6)], [((0, 1, 2, 3), 2), ((4, 5, 6, 7), 3)]]
TURNED = 2 * P


def load_scale_rows(queues, plane, rows):
    for r in range(4):
        queues[r].dma_start(
            out=plane[r:P:32, :, :].bitcast(I32),
            in_=rows[:, r:16:4, :].rearrange("g q c -> q g c").bitcast(I32),
        )


def fill_scale_plane(queues, plane, rows):
    words = rows.bitcast(I32)
    for q in range(4):
        queues[q].dma_start(
            out=plane[32 * q : 32 * q + 32, :].bitcast(I32),
            in_=words[4 * q : 4 * q + 4, :].unsqueeze(0).broadcast_to([8, 4, words.shape[1]]),
        )


def tile_moe_adp_relu_kernel(
    tc, x_words, x_scales, w_words, w_scales, wa_words, wa_scales, wb_words, wb_scales, gate, offs, pos1, pos2, out
):
    nc = tc.nc
    with ExitStack() as ctx:
        keep = ctx.enter_context(tc.tile_pool(name="keep", bufs=1))
        psum = ctx.enter_context(tc.psum_pool(name="psum", bufs=1))

        def bank(number, shape, name):
            return psum.tile(shape, F32, name=name, tag="bank%d" % number)

        offs_t = keep.tile([P, SLOTS // LIST_COLUMN], U16, name="offs_t")
        pos_t = [keep.tile([P, T // LIST_COLUMN], U16, name="pos%d_t" % r) for r in (1, 2)]
        x_w = keep.tile([P, T], U32, name="x_w", align_bytes=64)
        x_plane = keep.tile([P, T], U8, name="x_plane", align_bytes=64)
        w_w = keep.tile([P, N], U32, name="w_w", align_bytes=64)
        w_plane = keep.tile([P, N], U8, name="w_plane", align_bytes=64)
        wa_loads = range(E // LOAD_ADAPTERS)
        wa_planes = [keep.tile([P, LOAD_ADAPTERS, H], U8, name="wa_plane%d" % g, align_bytes=64) for g in wa_loads]
        wb_plane = keep.tile([P, E, N], U8, name="wb_plane", align_bytes=64)
        wb_w = keep.tile([P, E, 2 * N], U8, name="wb_w", align_bytes=64)
        gate_t = keep.tile([P, 2, T], F32, name="gate_t")
        ident = keep.tile([P, P], F32, name="ident")
        wa_w = [keep.tile([P, LOAD_ADAPTERS, 2 * H], U8, name="wa_w%d" % g, align_bytes=64) for g in wa_loads]
        wa_w_of = [wa_w[e // LOAD_ADAPTERS][:, e % LOAD_ADAPTERS, :] for e in range(E)]
        wa_plane_of = [wa_planes[e // LOAD_ADAPTERS][:, e % LOAD_ADAPTERS, :] for e in range(E)]
        both_queues = (nc.sync, nc.scalar, nc.sync, nc.scalar)
        sync_queue = (nc.sync,) * 4

        def load_wa_words(g, queue):
            rows = wa_words[LOAD_ADAPTERS * g : LOAD_ADAPTERS * (g + 1), 0].rearrange("e p c -> p e c")
            queue.dma_start(out=wa_w[g][:].bitcast(I32), in_=rows.bitcast(I32))

        def load_wa_plane(g):
            load_scale_rows(sync_queue, wa_planes[g], wa_scales[LOAD_ADAPTERS * g : LOAD_ADAPTERS * (g + 1), 0])

        for plane in wa_planes:
            nc.vector.memset(plane[:].bitcast(I32), 0)
        nc.vector.memset(wb_plane[:].bitcast(I32), 0)
        make_identity(nc, ident[:])

        nc.sync.dma_start(offs_t[:], offs)
        fill_scale_plane(both_queues, x_plane, x_scales[0])
        nc.scalar.dma_start(out=x_w[:].bitcast(I32), in_=x_words[0].rearrange("p t d -> p (t d)").bitcast(I32))
        load_wa_words(0, nc.scalar)
        load_wa_plane(0)
        load_wa_words(1, nc.sync)
        load_wa_plane(1)
        nc.sync.dma_start(out=wb_w[:].bitcast(I32), in_=wb_words[:, 0].rearrange("e p c -> p e c").bitcast(I32))
        load_scale_rows(sync_queue, wb_plane, wb_scales[:, 0])
        nc.sync.dma_start(out=w_w[:].bitcast(I32), in_=w_words[0].rearrange("p n d -> p (n d)").bitcast(I32))
        fill_scale_plane(sync_queue, w_plane, w_scales[0])
        nc.sync.dma_start(out=gate_t[:], in_=gate.rearrange("r p t -> p r t"))
        nc.sync.dma_start(pos_t[1][:], pos2)
        nc.sync.dma_start(pos_t[0][:], pos1)

        slot_w, slot_plane = {}, {}

        def gather(source, dtype, slots, name, e0, e1):
            picked = keep.tile([P, (e1 - e0) * C], dtype, name="%s%d" % (name, e0), align_bytes=64)
            entries = offs_t[:, e0 * C // LIST_COLUMN : e1 * C // LIST_COLUMN]
            nc.vector.tensor_copy(picked[:], source[:].indirect(entries))
            for e in range(e0, e1):
                slots[e] = picked[:, (e - e0) * C : (e - e0 + 1) * C]

        for e0, e1 in GATHER_GROUPS:
            gather(x_plane, U8, slot_plane, "slot_plane", e0, e1)
            gather(x_w, U32, slot_w, "slot_w", e0, e1)

        sorted_w, sorted_plane = {}, {}
        for e in DIRECT:
            sorted_w[e] = keep.tile([P, H], U16, name="sorted_w%d" % e, align_bytes=64)
            sorted_plane[e] = keep.tile([P, H], U8, name="sorted_plane%d" % e, align_bytes=64)
            for dst, src in ((sorted_w[e], wa_w_of[e].bitcast(U16)), (sorted_plane[e], wa_plane_of[e])):
                nc.gpsimd.tensor_copy(dst[:].rearrange("p (d m) -> p d m", d=4), src.rearrange("p (m d) -> p d m", d=4))

        def relu(e, dst, src):
            if e in VECTOR_RELU:
                nc.vector.tensor_scalar_max(dst, src, 0.0)
            else:
                nc.scalar.activation(dst, src, RELU)

        h_rows = {}

        def turned_layer(e, number):
            sums = bank(number, [P, H], "h_sums%d" % e)
            nc.tensor.matmul_mx(
                out=sums[:],
                lhsT=slot_w[e].bitcast(FP8X4),
                lhsT_scale=slot_plane[e],
                rhs=wa_w_of[e].bitcast(FP4X4),
                rhs_scale=wa_plane_of[e],
                start=True,
                stop=True,
            )
            h_rows[e] = keep.tile([P, H], BF16, name="h_rows%d" % e, align_bytes=64)
            dst = h_rows[e][:].rearrange("s (u p d) -> s u p d", u=2, d=2)
            relu(e, dst, sums[:].rearrange("s (p u d) -> s u p d", u=2, d=2))

        h_ready = {DIRECT: keep.tile([P, len(DIRECT) * C * 4], BF16, name="h_direct", align_bytes=64)}

        def direct_layer(e, number):
            sums = bank(number, [P, 4, C], "h_sums%d" % e)
            for d in range(4):
                nc.tensor.matmul_mx(
                    out=sums[:, d, :],
                    lhsT=sorted_w[e][:, d * P : (d + 1) * P].bitcast(FP4X4),
                    lhsT_scale=sorted_plane[e][:, d * P : (d + 1) * P],
                    rhs=slot_w[e].bitcast(FP8X4),
                    rhs_scale=slot_plane[e],
                    start=True,
                    stop=True,
                )
            x = DIRECT.index(e)
            dst = h_ready[DIRECT][:, x * C * 4 : (x + 1) * C * 4].rearrange("p (s d) -> p s d", d=4)
            relu(e, dst, sums[:].rearrange("p d s -> p s d"))

        def turn(group, number, copy):
            count = len(group)
            pairs = bank(number, [P, 2, 2, C], "h_pairs%d" % group[0])
            for x, e in enumerate(group):
                words = h_rows[e][:].bitcast(F32)
                for u in range(2):
                    nc.tensor.transpose(pairs[:, x, u, :], words[:, u * P : (u + 1) * P], ident[:])
            h_ready[group] = keep.tile([P, count * C * 4], BF16, name="h_turned%d" % group[0], align_bytes=64)
            copy(
                h_ready[group][:].bitcast(F32).rearrange("p (x s u) -> p x s u", x=count, u=2),
                pairs[:, 0:count, :, :].rearrange("p x u s -> p x s u"),
            )

        h_w, h_plane, y_sums = {}, {}, {}

        def second_layer(adapters, half):
            for e in adapters:
                members, number = [g for g in Y_GROUPS[half] if e in g[0]][0]
                if (members, half) not in y_sums:
                    y_sums[(members, half)] = bank(number, [P, len(members) * C], "y_sums%d_%d" % (half, members[0]))
                x = members.index(e)
                nc.tensor.matmul_mx(
                    out=y_sums[(members, half)][:, x * C : (x + 1) * C],
                    lhsT=wb_w[:, e, 2 * P * half : 2 * P * (half + 1)].bitcast(FP4X4),
                    lhsT_scale=wb_plane[:, e, P * half : P * (half + 1)],
                    rhs=h_w[e].bitcast(FP8X4),
                    rhs_scale=h_plane[e],
                    start=True,
                    stop=True,
                )

        def quantize_and_multiply(group):
            words = keep.tile([P, len(group) * C], U32, name="h_w%d" % group[0], align_bytes=64)
            plane = keep.tile([P, len(group) * C], U8, name="h_plane%d" % group[0], align_bytes=64)
            nc.vector.quantize_mx(out=words[:].bitcast(FP8X4), scales=plane[:], in_=h_ready[group][:])
            for x, e in enumerate(group):
                h_w[e] = words[:, x * C : (x + 1) * C]
                h_plane[e] = plane[:, x * C : (x + 1) * C]
            second_layer(group, 0)

        y = [keep.tile([P, SLOTS], F32, name="y%d" % half) for half in range(2)]

        def y_out(half, index, copy):
            members = Y_GROUPS[half][index][0]
            step = members[1] - members[0] if len(members) > 1 else 1
            copy(
                y[half][:].rearrange("p (e c) -> p e c", c=C)[:, members[0] : members[-1] + 1 : step, :],
                y_sums[(members, half)][:].rearrange("p (e c) -> p e c", c=C),
            )

        for e in range(1, E - 1):
            turned_layer(e, e - 1)
        turn((1, 2), 2, nc.vector.tensor_copy)
        turn((3, 4), 0, nc.scalar.copy)
        quantize_and_multiply((1, 2))
        direct_layer(0, 3)
        direct_layer(E - 1, 6)
        quantize_and_multiply((3, 4))
        turn((5,), BANKS - 1, nc.scalar.copy)
        turn((6,), 2, nc.scalar.copy)
        quantize_and_multiply(DIRECT)
        quantize_and_multiply((5,))
        quantize_and_multiply((6,))
        y_out(0, 0, nc.scalar.copy)
        y_out(0, 1, nc.vector.tensor_copy)
        y_out(0, 2, nc.scalar.copy)
        y_out(0, 3, nc.scalar.copy)
        second_layer(range(E), 1)

        def frozen(sums, tokens, rows, token_major):
            a = (x_w[:, tokens].bitcast(FP8X4), x_plane[:, tokens])
            b = (w_w[:, rows].bitcast(FP8X4), w_plane[:, rows])
            lhs, rhs = (a, b) if token_major else (b, a)
            nc.tensor.matmul_mx(out=sums, lhsT=lhs[0], lhsT_scale=lhs[1], rhs=rhs[0], rhs_scale=rhs[1], start=True, stop=True)

        def transpose(dst, src, start, stop):
            nc.tensor.matmul(dst, lhsT=src, rhs=ident[:], is_transpose=True, start=start, stop=stop)

        blocks = [slice(j * P, (j + 1) * P) for j in range(TURNED // P)]
        halves = [slice(half * P, (half + 1) * P) for half in range(2)]
        rest = slice(TURNED, T)
        base_turned = bank(BANKS - 1, [P, 2, N], "base_turned")
        for j in range(2):
            frozen(base_turned[:, j, :], blocks[j], slice(0, N), True)
        base_rest = bank(0, [P, 2, T - TURNED], "base_rest")
        for half in range(2):
            frozen(base_rest[:, half, :], rest, halves[half], False)
        y_out(1, 0, nc.scalar.copy)
        y_out(1, 1, nc.scalar.copy)

        step = P // LIST_COLUMN
        first_low = keep.tile([P, TURNED], F32, name="first_low", tag="low_then_base")
        first_high = [keep.tile([P, P], F32, name="first_high%d" % j) for j in range(2)]
        first_rest = keep.tile([P, 2, T - TURNED], F32, name="first_rest")
        second = keep.tile([P, 2, T], F32, name="second")
        nc.scalar.activation(first_low[:], y[0][:].indirect(pos_t[0][:, 0 : 2 * step]), COPY)
        for j in range(2):
            nc.scalar.activation(first_high[j][:], y[1][:].indirect(pos_t[0][:, j * step : (j + 1) * step]), COPY)
        partial = keep.tile([P, 2, T - TURNED], F32, name="partial")

        def fetch_second(half):
            nc.vector.tensor_tensor(second[:, half, :], y[half][:].indirect(pos_t[1][:]), gate_t[:, 1, :], MULT)

        def fetch_first(half):
            entries = pos_t[0][:, 2 * step : T // LIST_COLUMN]
            nc.vector.tensor_tensor(first_rest[:, half, :], y[half][:].indirect(entries), gate_t[:, 0, rest], MULT)

        def add_base(half):
            nc.vector.tensor_tensor(partial[:, half, :], base_rest[:, half, :], second[:, half, rest], ADD)

        fetch_second(0)
        fetch_first(0)
        fetch_second(1)
        add_base(0)
        fetch_first(1)
        add_base(1)

        gate_turned = bank(1, [P, 2, P], "gate_turned")
        for j in range(2):
            transpose(gate_turned[:, j, :], gate_t[:, 0, blocks[j]], True, True)
        turned = [bank((4, 5)[j], [P, 2, P], "turned%d" % j) for j in range(2)]
        for j in range(2):
            transpose(turned[j][:, 0, :], first_low[:, blocks[j]], True, True)
        for j in range(2):
            transpose(turned[j][:, 1, :], first_high[j][:], True, True)
        base_t = keep.tile([P, 2, N], F32, name="base_t", tag="low_then_base")
        nc.scalar.copy(base_t[:], base_turned[:])
        gate_columns = keep.tile([P, 2], F32, name="gate_columns")
        nc.scalar.copy(gate_columns[:], gate_turned[:, :, 0])
        totals = [bank((6, 2)[half], [P, 2, P], "total%d" % half) for half in range(2)]
        for half in range(2):
            for j in range(2):
                transpose(totals[half][:, j, :], base_t[:, j, halves[half]], j == 0, False)
        for j in range(2):
            gated = keep.tile([P, N], F32, name="gated%d" % j)
            nc.scalar.activation(gated[:], turned[j][:].rearrange("p h n -> p (h n)"), COPY, scale=gate_columns[:, j : j + 1])
            for half in range(2):
                transpose(totals[half][:, j, :], gated[:, halves[half]], False, j == 1)

        for half in range(2):
            result = keep.tile([P, T - TURNED], F32, name="result_rest%d" % half)
            nc.vector.tensor_tensor(result[:], partial[:, half, :], first_rest[:, half, :], ADD)
            nc.sync.dma_start(out=out[halves[half], rest], in_=result[:])
        for half in range(2):
            result = keep.tile([P, TURNED], F32, name="result_turned%d" % half)
            nc.vector.tensor_tensor(result[:], totals[half][:].rearrange("p j t -> p (j t)"), second[:, half, 0:TURNED], ADD)
            nc.sync.dma_start(out=out[halves[half], 0:TURNED], in_=result[:])
